import numpy as np, ml_dtypes
CORES = [8,136,40,168]
N = 4
BF = ml_dtypes.bfloat16
def gentries(a):
    return np.ascontiguousarray(a.reshape(8, 16, -1).transpose(0, 2, 1)).reshape(8, -1)
def gtable(e):
    e = np.asarray(e); return np.ascontiguousarray(e.reshape(8, -1, 16).transpose(0, 2, 1)).reshape(128, -1).astype(np.int32)
S, CAP, H = 2048, 576, 2
def channel(rng):
    v = rng.integers(-45, 46, (N, 128, S)) + rng.integers(-24, -4, (N, 128, 1))
    return np.clip(v, -63, 63).astype(np.float32).astype(BF)
def counts(rng):
    n = np.full((N, N), S // N, np.int64)
    for i in range(4 * N):
        q = rng.choice(N, 2, replace=False); r = rng.choice(N, 2, replace=False)
        d = min(CAP - n[q[0], r[0]], CAP - n[q[1], r[1]], n[q[0], r[1]], n[q[1], r[0]], (CAP - S // N) // 3 + 1)
        d = rng.integers(0, d + 1); n[q[0], r[0]] += d; n[q[1], r[1]] += d; n[q[0], r[1]] -= d; n[q[1], r[0]] -= d
    return n
def slots(rng, n, runs=False):
    sa = np.zeros((N, 8, S), np.int32); sb = np.zeros((N, 8, S), np.int32)
    def places():
        return rng.permutation(S) if not runs else np.arange(S) if rng.integers(0, 2) else np.arange(S)[::-1]
    for g in range(8):
        pa = [places() for q in range(N)]; pb = [places() for r in range(N)]
        for q in range(N):
            for r in range(N):
                m = int(n[g][q, r]); i = int(np.sum(n[g][q, :r])); j = int(np.sum(n[g][:q, r]))
                c = np.arange(m) if runs else rng.permutation(CAP)[:m]
                sa[q, g, pa[q][i:i + m]] = r * CAP + c; sb[r, g, pb[r][j:j + m]] = q * CAP + c
    return {"sa": np.stack([gtable(v) for v in sa]), "sb": np.stack([gtable(v) for v in sb])}
def setup_inputs(rng):
    d = {"a": channel(rng), "b": channel(rng)}
    d.update(slots(rng, [counts(rng) for g in range(8)])); return d
def setup_inputs_full(rng):
    d = setup_inputs(rng); n = np.full((8, N, N), S // N, np.int64); q = np.arange(N)
    for g in range(8):
        k = rng.integers(1, N); l = (k + rng.integers(1, N)) % N
        n[g, q, (q + k) % N] += CAP - S // N; n[g, q, (q + l) % N] -= CAP - S // N
    d.update(slots(rng, n)); return d
def setup_inputs_runs(rng):
    d = setup_inputs(rng); d.update(slots(rng, [counts(rng) for g in range(8)], True)); return d
def setup_inputs_ends(rng):
    d = setup_inputs(rng); vals = np.array([-63, -63, -63, -63, -15, -1, 0, 1, 15, 63]); k = rng.permutation(128)
    for name in ("a", "b"):
        v = rng.choice(vals, (N, 128, S)); v[:, k[:64]] = np.repeat(rng.choice(vals, (N, 64, S // 32)), 32, axis=2)
        v[:, k[0]] = 63; v[:, k[1]] = -63; v[:, k[2]] = 0
        d[name] = v.astype(np.float32).astype(BF)
    return d
def setup_inputs_spread(rng):
    d = setup_inputs(rng)
    for name in ("a", "b"):
        amp = 2 ** rng.integers(0, 7, (N, 1, S)) - 1
        v = np.minimum(np.floor(rng.random((N, 128, S)) ** 3 * (2 * amp + 1)), 2 * amp) - amp
        d[name] = v.astype(np.float32).astype(BF)
    return d
def check_inputs(d):
    bad = []
    try:
        for k in ("a", "b"):
            v = np.asarray(d[k]).astype(np.float64)
            if v.shape != (N, 128, S) or not np.isfinite(v).all() or (v != np.floor(v)).any() or (np.abs(v) > 63).any(): bad.append(k)
        used = []
        for k in ("sa", "sb"):
            v = np.asarray(d[k])
            if v.shape != (N, 128, S // 16) or v.min() < 0 or v.max() >= N * CAP:
                bad.append(k); continue
            u = np.zeros((N, 8, N * CAP), bool)
            for r in range(N): u[r][np.arange(8)[:, None], gentries(v[r])] = True
            if (np.sum(u, axis=-1) != S).any(): bad.append(k + " repeats")
            used.append(u.reshape(N, 8, N, CAP))
        if len(used) == 2 and (used[0] != used[1].transpose(2, 1, 0, 3)).any(): bad.append("slots of pairs")
    except Exception:
        bad.append("inputs")
    return bad
def partners(sa, sb):
    g = np.arange(8)[:, None]; inv = np.zeros((N, 8, N * CAP), np.int64); src = np.zeros((8, N * S), np.int64)
    for q in range(N): inv[q][g, gentries(sa[q])] = np.arange(S)
    for r in range(N):
        s = gentries(sb[r]).astype(np.int64); q = s // CAP
        src[:, r * S:(r + 1) * S] = q * S + inv[q, g, r * CAP + s - q * CAP]
    return src
def carry(e, src, back):
    x = np.ascontiguousarray(e.reshape(N, 8, 16, S).transpose(1, 2, 0, 3)).reshape(8, 16, N * S); z = np.zeros_like(x)
    for g in range(8):
        if back: z[g][:, src[g]] = x[g]
        else: z[g] = x[g][:, src[g]]
    return np.ascontiguousarray(z.reshape(8, 16, N, S).transpose(2, 0, 1, 3)).reshape(N, 128, S)
def scan(v, back):
    x = np.ascontiguousarray(np.moveaxis(v, -1, 0)); z = np.zeros_like(x); s = np.zeros_like(x[0])
    for t in (range(S - 1, -1, -1) if back else range(S)):
        s = np.maximum(s + x[t], 0); z[t] = s
    return np.moveaxis(z, 0, -1)
def extrinsic(v):
    e = np.full(v.shape, -15, np.int64)
    e[..., 1:] += np.minimum(scan(v, False), 15)[..., :-1]
    e[..., :-1] += np.minimum(scan(v, True), 15)[..., 1:]
    return e
def reference(a, b, sa, sb):
    src = partners(sa, sb)
    ca = a.astype(np.float32).astype(np.int64); cb = b.astype(np.float32).astype(np.int64)
    prior = np.zeros((N, 128, S), np.int64)
    for h in range(H // 2):
        prior = carry(extrinsic(ca + prior), src, False)
        prior = carry(extrinsic(cb + prior), src, True)
    return {"y": (ca + prior).astype(np.float32).astype(BF)}

@@ -1,0 +1,360 @@
+from concourse.mybir import AluOpType as Alu, ActivationFunctionType as Act
+
+N, S, CAP = 4, 2048, 576
+SLOTS = N * CAP
+HALF = CAP // 2
+KB = CAP // 16
+WW = 4096
+BASE = 32
+KA = 72
+KB0, KB1 = 40, 108
+NV1, NV2 = 1216, 1280
+CUT = 768
+NI = 16 * max(KA, KB1)
+SCALES = {"up": 32.0, "un": -32.0, "lp": 1.0, "ln": -1.0}
+MID = 192.0
+
+SCRATCH = {
+    "A": ("sbuf", [128, S], "bfloat16"), "B": ("sbuf", [128, S], "bfloat16"),
+    "la": ("sbuf", [128, 128], "int32"), "lb": ("sbuf", [128, 128], "int32"),
+    "t1": ("sbuf", [128, 128], "int32"), "t2": ("sbuf", [128, 128], "int32"),
+    "t3": ("sbuf", [128, 128], "int32"), "t4": ("sbuf", [128, 128], "int32"),
+    "posa": ("sbuf", [128, 128], "uint16"), "posb": ("sbuf", [128, 128], "uint16"),
+    "ua": ("sbuf", [128, 128], "uint16"), "ub": ("sbuf", [128, 128], "uint16"),
+    "Z": ("sbuf", [128, WW // 16], "float32"), "zer": ("sbuf", [128, S], "bfloat16"),
+    "num": ("sbuf", [128, NI], "float32"),
+    "Wav": ("sbuf", [128, WW], "float32"), "Was": ("sbuf", [128, WW], "float32"),
+    "Wbv": ("sbuf", [128, WW], "float32"), "Wbs": ("sbuf", [128, WW], "float32"),
+    "Oav": ("sbuf", [128, WW // 16], "float32"), "Oas": ("sbuf", [128, WW // 16], "float32"),
+    "Obv": ("sbuf", [128, WW // 16], "float32"), "Obs": ("sbuf", [128, WW // 16], "float32"),
+    "Osa": ("sbuf", [128, N * KB], "float32"), "Osb": ("sbuf", [128, N * KB], "float32"),
+    "inva": ("sbuf", [128, N * KB], "uint16"), "invb": ("sbuf", [128, N * KB], "uint16"),
+    "Fn": ("sbuf", [128, S], "bfloat16"), "Bn": ("sbuf", [128, S], "bfloat16"),
+    "FG": ("sbuf", [128, SLOTS], "bfloat16"), "RB": ("sbuf", [128, SLOTS], "bfloat16"),
+    "S1": ("sbuf", [128, N * HALF], "float16"), "S2": ("sbuf", [128, N * HALF], "float16"),
+    "X1": ("sbuf", [128, N * HALF], "float16"), "X2": ("sbuf", [128, N * HALF], "float16"),
+    "U": ("sbuf", [128, N * HALF], "bfloat16"), "V": ("sbuf", [128, N * HALF], "bfloat16"),
+    "R1": ("sbuf", [128, SLOTS], "bfloat16"), "R2": ("sbuf", [128, SLOTS], "bfloat16"),
+    "L": ("sbuf", [128, S], "bfloat16"), "Y": ("sbuf", [128, S], "bfloat16"),
+    "G": ("sbuf", [128, S - min(NV1, NV2)], "bfloat16"),
+}
+for _n in SCALES:
+    SCRATCH["c" + _n] = ("sbuf", [128, 128], "bfloat16")
+    SCRATCH[_n] = ("sbuf", [128, 128], "bfloat16")
+for _n in ("P0", "P1", "P2", "P3", "Q1", "Q2", "Q3"):
+    SCRATCH[_n] = ("psum", [128, 512], "float32")
+SEMAPHORES = ["sent"] + ["a%d_%d" % (h, k) for h in (1, 2) for k in range(1, N)] + ["e%d" % i for i in range(140)]
+
+
+def new_plan():
+    return {"ops": [], "acc": [], "known": {}, "groups": {}}
+
+
+def add(plan, q, fn, reads=(), writes=(), inc=1, sem=None, group=None):
+    ops = plan["ops"]
+    me = len(ops)
+    deps = set()
+    for (buf, lo, hi, who, wr) in plan["acc"]:
+        for (b2, l2, h2) in writes:
+            if buf == b2 and lo < h2 and l2 < hi:
+                deps.add(who)
+        if wr:
+            for (b2, l2, h2) in reads:
+                if buf == b2 and lo < h2 and l2 < hi:
+                    deps.add(who)
+    known = plan["known"].setdefault(q, set())
+    waits = []
+    for d in sorted(deps, reverse=True):
+        gd = ops[d]["group"]
+        if d in known or (gd is not None and gd == group):
+            continue
+        members = plan["groups"][gd] if gd is not None else [d]
+        waits.append(members[0])
+        for m in members:
+            known |= ops[m]["knows"]
+    ops.append({"q": q, "fn": fn, "waits": waits, "knows": set(known) | {me}, "inc": inc, "sem": sem, "group": group})
+    if group is not None:
+        plan["groups"].setdefault(group, []).append(me)
+    for (b2, l2, h2) in reads:
+        plan["acc"].append((b2, l2, h2, me, False))
+    for (b2, l2, h2) in writes:
+        plan["acc"].append((b2, l2, h2, me, True))
+
+
+def emit(plan, queues, T):
+    ops = plan["ops"]
+    needed = set()
+    for op in ops:
+        needed |= set(op["waits"])
+    sems, count = {}, 0
+    for i, op in enumerate(ops):
+        if op["sem"] is not None:
+            sems[i] = (T.sem[op["sem"][0]], op["sem"][1])
+        elif i in needed:
+            members = plan["groups"][op["group"]] if op["group"] is not None else [i]
+            for m in members:
+                sems[m] = (T.sem["e%d" % count], op["inc"] * len(members))
+            count += 1
+    for i, op in enumerate(ops):
+        if op["q"] is None:
+            continue
+        eng = queues[op["q"]]
+        for d in op["waits"]:
+            eng.wait_ge(sems[d][0], sems[d][1])
+        if op["fn"] is not None:
+            ins = op["fn"](eng)
+            if i in sems:
+                ins.then_inc(sems[i][0], op["inc"])
+
+
+def rank_program(g, core, T, topo):
+    q = T.rank_of(core)
+    if q is None:
+        return
+    plan = new_plan()
+    queues = {"g": g, "v": g.vector, "s": g.scalar, "y": g.sync, "t": g.tensor}
+    outgoing = sum(len(topo.engines(core, c)) for c in T.cores if c != core)
+
+    def whole(name):
+        return (name, 0, T[name].shape[1])
+
+    def dma(queue, out, in_, reads, writes):
+        add(plan, queue, lambda e: e.dma_start(out, in_), reads, writes, inc=16)
+
+    def load(queue, dst, src):
+        dma(queue, T[dst][:], src[:], [], [whole(dst)])
+
+    def fill(queue, w):
+        dma(queue, T[w][0:128:16, :], T.Z[:], [whole("Z")], [whole(w)])
+
+    def regroup(w, o):
+        dma("y", T[o][:], T[w][0:128:16, :], [whole(w)], [whole(o)])
+
+    def memset(name, lo, hi, val):
+        add(plan, "v", lambda e: e.memset(T[name][:, lo:hi], val), [], [(name, lo, hi)])
+
+    def numbers(lo, hi):
+        add(plan, "g", lambda e: e.iota(T.num[:, lo:hi], [[1, hi - lo]], BASE + lo, 0, allow_small_or_imprecise_dtypes=True),
+            [], [("num", lo, hi)])
+
+    def identity(name):
+        add(plan, "g", lambda e: e.affine_select(T[name][:], T["c" + name][:], [[-1, 128]], Alu.is_equal, 0.0, 0, 1),
+            [whole("c" + name)], [whole(name)])
+
+    def affine(queue, out, olo, src, lo, n, mul, plus):
+        o, i = T[out][:, olo:olo + n], T[src][:, lo:lo + n]
+        if queue == "v":
+            fn = lambda e: e.tensor_scalar(o, i, mul, plus, Alu.mult, Alu.add)
+        else:
+            fn = lambda e: e.activation(o, i, Act.Identity, bias=plus, scale=mul)
+        add(plan, queue, fn, [(src, lo, lo + n)], [(out, olo, olo + n)])
+
+    def narrow(out, src):
+        add(plan, "v", lambda e: e.tensor_copy(T[out][:], T[src][:]), [whole(src)], [whole(out)])
+
+    def positions(lst, ta, tb, pos):
+        add(plan, "v", lambda e: e.tensor_scalar(T[ta][:], T[lst][:], WW + 1, None, Alu.mult), [whole(lst)], [whole(ta)])
+        add(plan, "v", lambda e: e.tensor_scalar(T[tb][:], T[ta][:], 4, WW - 1, Alu.logical_shift_right, Alu.bitwise_and),
+            [whole(ta)], [whole(tb)])
+        narrow(pos, tb)
+
+    def scatter_s(w, pos, c, d):
+        add(plan, "s", lambda e: e.activation(T[w][:, 0:WW].indirect(T[pos][:, c:d]), T.num[:, 16 * c:16 * d], Act.Silu),
+            [whole(pos), ("num", 16 * c, 16 * d)], [whole(w)])
+
+    def scatter_v(w, pos, c, d):
+        add(plan, "v", lambda e: e.tensor_scalar(T[w][:, 0:WW].indirect(T[pos][:, c:d]), T.num[:, 0:16 * (d - c)],
+                                                 1.0, float(16 * c), Alu.mult, Alu.add),
+            [whole(pos), ("num", 0, 16 * (d - c))], [whole(w)])
+
+    def combine(ov, os_, osum, inv, lo, hi):
+        add(plan, "v", lambda e: e.tensor_tensor(T[osum][:, lo:hi], T[ov][:, lo:hi], T[os_][:, lo:hi], Alu.add),
+            [whole(ov), whole(os_)], [(osum, lo, hi)])
+        add(plan, "v", lambda e: e.tensor_scalar(T[inv][:, lo:hi], T[osum][:, lo:hi], 0.25 - BASE, 0.0, Alu.add, Alu.max),
+            [(osum, lo, hi)], [(inv, lo, hi)])
+
+    def scan_b(src):
+        add(plan, "v", lambda e: e.tensor_tensor_scan(T.Bn[:, S - 2::-1], T[src][:, S - 1:0:-1], T.zer[:, 0:S - 1], 0.0,
+                                                      Alu.add, Alu.max),
+            [whole(src), whole("zer")], [("Bn", 0, S - 1)])
+
+    def scan_f(src):
+        add(plan, "v", lambda e: e.tensor_tensor_scan(T.Fn[:, 1:S], T[src][:, 0:S - 1], T.zer[:, 0:S - 1], 0.0,
+                                                      Alu.add, Alu.max),
+            [whole(src), whole("zer")], [("Fn", 1, S)])
+
+    def below(out, src, inv, lo, hi):
+        off = T[inv][:, lo // 16:hi // 16]
+        add(plan, "s", lambda e: e.activation(T[out][:, lo:hi], T[src][:, 0:S].indirect(off), Act.Relu, bias=15.0, scale=-1.0),
+            [whole(src), (inv, lo // 16, hi // 16)], [(out, lo, hi)])
+
+    def capped(inv, lo, hi):
+        off = T[inv][:, lo // 16:hi // 16]
+        add(plan, "v", lambda e: e.tensor_scalar(T.FG[:, lo:hi], T.Fn[:, 0:S].indirect(off), 15.0, None, Alu.min),
+            [whole("Fn"), (inv, lo // 16, hi // 16)], [("FG", lo, hi)])
+
+    def matmul(bank, n, mat, src, lo, start, stop, group):
+        add(plan, "t", lambda e: e.matmul(T[bank][:, 0:n], T[mat][:], T[src][:, lo:lo + n], start, stop),
+            [whole(mat), (src, lo, lo + n)], [whole(bank)], group=group)
+
+    def send(h, k):
+        r = (q + k) % N
+        dst = T.cores[r]
+        rid, pid = topo.addr(dst, core)
+        sbuf = "S%d" % h
+
+        def fn(e):
+            e.remote_dma(T["X%d" % h][:, q * HALF:(q + 1) * HALF], T[sbuf][:, r * HALF:(r + 1) * HALF],
+                         T.sem["a%d_%d" % (h, k)], T.sem.sent, pid, rid, topo.mask(core, dst))
+        add(plan, "g", fn, [(sbuf, r * HALF, (r + 1) * HALF)], [])
+
+    def exchange(h, inv, steps, extra=None):
+        steps = [(w[0], int(w[1])) for w in steps.split()]
+        by_s = [k for what, k in steps if what == "s"]
+        terms = {}
+
+        def term(k, mat, src, c):
+            i = terms.get(k, 0)
+            terms[k] = i + 1
+            matmul("Q%d" % k, HALF, mat, src, c, i == 0, i == 3, ("pack", h, k))
+        for what, k in steps:
+            r = (q + k) % N
+            lo, mid, hi = r * CAP, r * CAP + HALF, (r + 1) * CAP
+            if what in "bcd":
+                below("RB", "Bn", inv, mid if what == "d" else lo, mid if what == "c" else hi)
+                if what != "d":
+                    term(k, "un", "RB", lo)
+                if what != "c":
+                    term(k, "ln", "RB", mid)
+            elif what == "s":
+                below("FG", "Fn", inv, lo, mid)
+                term(k, "un", "FG", lo)
+            elif what == "u":
+                capped(inv, lo, mid)
+                term(k, "up", "FG", lo)
+            elif what == "l":
+                capped(inv, mid, hi)
+                term(k, "lp", "FG", mid)
+            elif what == "x":
+                extra()
+            else:
+                affine("v", "S%d" % h, r * HALF, "Q%d" % k, 0, HALF, 1.0, 15.0 * 32 if k in by_s else 0.0)
+                send(h, k)
+
+    def own(h, inv, by_tensor):
+        lo, hi, out = q * CAP, (q + 1) * CAP, "R%d" % h
+        below("RB", "Bn", inv, lo, hi)
+        capped(inv, lo, hi)
+        if not by_tensor:
+            add(plan, "v", lambda e: e.tensor_tensor(T[out][:, lo:hi], T.FG[:, lo:hi], T.RB[:, lo:hi], Alu.subtract),
+                [("FG", lo, hi), ("RB", lo, hi)], [(out, lo, hi)])
+            return
+        for k in range(2):
+            c, bank = lo + k * HALF, "Q%d" % (k + 1)
+            matmul(bank, HALF, "ln", "RB", c, True, False, ("own", h, k))
+            matmul(bank, HALF, "lp", "FG", c, False, True, ("own", h, k))
+            affine("s", out, c, bank, 0, HALF, 1.0, 0.0)
+
+    def unpack(h, helper):
+        x, out = "X%d" % h, "R%d" % h
+        for k in range(1, N):
+            r = (q - k) % N
+            c, lo = r * HALF, r * CAP
+            add(plan, None, None, [], [(x, c, c + HALF)], sem=("a%d_%d" % (h, k), len(topo.engines(T.cores[r], core))))
+            affine("v", "U", c, x, c, HALF, 1.0 / 32, MID)
+            affine("v", "V", c, "U", c, HALF, -32.0, 32 * MID)
+            affine(helper[k - 1], out, lo, "U", c, HALF, 1.0, -MID)
+            add(plan, "v", lambda e, c=c, lo=lo: e.tensor_tensor(T[out][:, lo + HALF:lo + CAP], T[x][:, c:c + HALF],
+                                                                 T.V[:, c:c + HALF], Alu.add),
+                [(x, c, c + HALF), ("V", c, c + HALF)], [(out, lo + HALF, lo + CAP)])
+
+    def channel_in(src, banks, nv):
+        nc = (S - nv) // 2
+        for k, p in enumerate(banks):
+            matmul(p, nc, "lp", src, nv + k * nc, True, False, p)
+
+    def gather_v(out, rbuf, off, src, lo, hi):
+        add(plan, "v", lambda e: e.tensor_tensor(T[out][:, lo:hi], T[rbuf][:, 0:SLOTS].indirect(T[off][:, lo // 16:hi // 16]),
+                                                 T[src][:, lo:hi], Alu.add),
+            [whole(rbuf), whole(off), (src, lo, hi)], [(out, lo, hi)])
+
+    def gather_s(out, rbuf, off, banks, nv):
+        nc = (S - nv) // 2
+        for k, p in enumerate(banks):
+            lo = nv + k * nc
+            add(plan, "s", lambda e, k=k, lo=lo: e.activation(
+                T.G[:, k * nc:(k + 1) * nc], T[rbuf][:, 0:SLOTS].indirect(T[off][:, lo // 16:(lo + nc) // 16]), Act.Copy),
+                [whole(rbuf), whole(off)], [("G", k * nc, (k + 1) * nc)])
+            matmul(p, nc, "lp", "G", k * nc, False, True, p)
+        for k, p in enumerate(banks):
+            lo = nv + k * nc
+            add(plan, "s", lambda e, p=p, lo=lo: e.activation(T[out][:, lo:lo + nc], T[p][:, 0:nc], Act.Copy),
+                [whole(p)], [(out, lo, lo + nc)])
+
+    def store(queue, lo, hi):
+        dma(queue, T.y[:, lo:hi], T.Y[:, lo:hi], [("Y", lo, hi)], [("y", lo, hi)])
+
+    load("y", "la", T.sa)
+    numbers(0, 16 * KA)
+    memset("Z", 0, WW // 16, 0.0)
+    fill("s", "Was")
+    fill("y", "Wav")
+    load("y", "lb", T.sb)
+    load("s", "A", T.a)
+    add(plan, "s", lambda e: e.activation(T.Bn[:, S - 1:S], T.Z[:, 0:1], Act.Silu), [whole("Z")], [("Bn", S - 1, S)])
+    fill("y", "Wbs")
+    memset("zer", 0, S, 0.0)
+    memset("Fn", 0, 1, 0.0)
+    for name in SCALES:
+        memset("c" + name, 0, 128, SCALES[name])
+        identity(name)
+    numbers(16 * KA, NI)
+
+    positions("la", "t1", "t2", "posa")
+    scatter_s("Was", "posa", 0, KA)
+    scatter_v("Wav", "posa", KA, 128)
+    positions("lb", "t3", "t4", "posb")
+    regroup("Wav", "Oav")
+    regroup("Was", "Oas")
+    load("y", "B", T.b)
+    fill("y", "Wbv")
+    scatter_s("Wbs", "posb", 0, KB0)
+    channel_in("A", ["P2", "P3"], NV2)
+    scan_b("A")
+    scan_f("A")
+    narrow("ub", "lb")
+    first = (q + 1) % N
+    combine("Oav", "Oas", "Osa", "inva", first * KB, (first + 1) * KB)
+
+    def others():
+        for lo, hi in (((first + 1) * KB, N * KB), (0, first * KB)):
+            if lo < hi:
+                combine("Oav", "Oas", "Osa", "inva", lo, hi)
+    exchange(1, "inva", "u1 c1 l1 d1 x0 p1 u2 b2 l2 b3 l3 p2 s3 p3", others)
+    channel_in("B", ["P0", "P1"], NV1)
+    own(1, "inva", False)
+
+    scatter_s("Wbs", "posb", KB0, KB1)
+    scatter_v("Wbv", "posb", KB1, 128)
+    regroup("Wbv", "Obv")
+    regroup("Wbs", "Obs")
+
+    unpack(1, "vvs")
+    gather_v("L", "R1", "ub", "B", 0, NV1)
+    gather_s("L", "R1", "ub", ["P0", "P1"], NV1)
+    combine("Obv", "Obs", "Osb", "invb", 0, N * KB)
+    scan_b("L")
+    scan_f("L")
+    exchange(2, "invb", "b1 u1 b2 l1 s2 l2 p1 l3 b3 p2 s3 p3")
+    own(2, "invb", True)
+    narrow("ua", "la")
+
+    unpack(2, "sss")
+    gather_v("Y", "R2", "ua", "A", 0, CUT)
+    gather_v("Y", "R2", "ua", "A", CUT, NV2)
+    gather_s("Y", "R2", "ua", ["P2", "P3"], NV2)
+    store("y", 0, CUT)
+    store("y", CUT, S)
+    add(plan, "y", None, [("y", 0, S)], [])
+    emit(plan, queues, T)
+    g.wait_ge(T.sem.sent, 2 * outgoing)

@@ -1,4 +1,5 @@
 from concourse.mybir import AluOpType as Alu, ActivationFunctionType as Act
+from concourse.bass import DstId, RemoteDMATransfer
 
 N, S, CAP = 4, 2048, 576
 SLOTS = N * CAP
@@ -6,13 +7,20 @@ HALF = CAP // 2
 KB = CAP // 16
 WW = 4096
 BASE = 32
-KA = 72
-KB0, KB1 = 40, 108
-NV1, NV2 = 1216, 1280
-CUT = 768
-NI = 16 * max(KA, KB1)
-SCALES = {"up": 32.0, "un": -32.0, "lp": 1.0, "ln": -1.0}
-MID = 192.0
+NI = 2048
+ROUND = 1.5 * 2.0 ** 28
+PARTS = {"": (0, CAP), "a": (0, HALF), "b": (HALF, CAP)}
+CFG = {
+    "KA": 70,
+    "KB0": 32, "KB1": 102,
+    "NV1": 1280, "NV2": 1280,
+    "N0": 704,
+    "CUTS": (512, 896),
+    "X1": "vF1a sB1a sB1b vF1b vF2a p1 sB2 vF2b sB3 vF3b p2 sF3a vF0a p3 sB0 vF0b c0 n0",
+    "X2": "sB1 vF1a vF1b p1 sB2 vF2a vF2b sF3a sB3 p2 vF3b p3 sB0 sF0 n0 r1 d0 r2",
+    "TURN1": "vvs", "TURN2": "vvs", "CB": 0,
+}
+SCALES = {"lp": 1.0, "ln": -1.0, "up": 32.0, "un": -32.0}
 
 SCRATCH = {
     "A": ("sbuf", [128, S], "bfloat16"), "B": ("sbuf", [128, S], "bfloat16"),
@@ -30,16 +38,17 @@ SCRATCH = {
     "Osa": ("sbuf", [128, N * KB], "float32"), "Osb": ("sbuf", [128, N * KB], "float32"),
     "inva": ("sbuf", [128, N * KB], "uint16"), "invb": ("sbuf", [128, N * KB], "uint16"),
     "Fn": ("sbuf", [128, S], "bfloat16"), "Bn": ("sbuf", [128, S], "bfloat16"),
-    "FG": ("sbuf", [128, SLOTS], "bfloat16"), "RB": ("sbuf", [128, SLOTS], "bfloat16"),
+    "F1": ("sbuf", [128, SLOTS], "bfloat16"), "B1": ("sbuf", [128, SLOTS], "bfloat16"),
+    "F2": ("sbuf", [128, SLOTS], "bfloat16"), "B2": ("sbuf", [128, SLOTS], "bfloat16"),
     "S1": ("sbuf", [128, N * HALF], "float16"), "S2": ("sbuf", [128, N * HALF], "float16"),
     "X1": ("sbuf", [128, N * HALF], "float16"), "X2": ("sbuf", [128, N * HALF], "float16"),
-    "U": ("sbuf", [128, N * HALF], "bfloat16"), "V": ("sbuf", [128, N * HALF], "bfloat16"),
+    "E1": ("sbuf", [128, SLOTS], "bfloat16"), "E2": ("sbuf", [128, SLOTS], "bfloat16"),
+    "U": ("sbuf", [128, N * HALF], "bfloat16"), "D2": ("sbuf", [128, SLOTS], "bfloat16"),
     "R1": ("sbuf", [128, SLOTS], "bfloat16"), "R2": ("sbuf", [128, SLOTS], "bfloat16"),
     "L": ("sbuf", [128, S], "bfloat16"), "Y": ("sbuf", [128, S], "bfloat16"),
-    "G": ("sbuf", [128, S - min(NV1, NV2)], "bfloat16"),
+    "G": ("sbuf", [128, 1024], "bfloat16"),
 }
 for _n in SCALES:
-    SCRATCH["c" + _n] = ("sbuf", [128, 128], "bfloat16")
     SCRATCH[_n] = ("sbuf", [128, 128], "bfloat16")
 for _n in ("P0", "P1", "P2", "P3", "Q1", "Q2", "Q3"):
     SCRATCH[_n] = ("psum", [128, 512], "float32")
@@ -111,9 +120,12 @@ def rank_program(g, core, T, topo):
     q = T.rank_of(core)
     if q is None:
         return
+    C = CFG
+    KA, KB0, KB1, NV1, NV2 = C["KA"], C["KB0"], C["KB1"], C["NV1"], C["NV2"]
     plan = new_plan()
     queues = {"g": g, "v": g.vector, "s": g.scalar, "y": g.sync, "t": g.tensor}
-    outgoing = sum(len(topo.engines(core, c)) for c in T.cores if c != core)
+    outgoing = [0]
+    packs = "p" in C["X1"] + C["X2"]
 
     def whole(name):
         return (name, 0, T[name].shape[1])
@@ -138,8 +150,8 @@ def rank_program(g, core, T, topo):
             [], [("num", lo, hi)])
 
     def identity(name):
-        add(plan, "g", lambda e: e.affine_select(T[name][:], T["c" + name][:], [[-1, 128]], Alu.is_equal, 0.0, 0, 1),
-            [whole("c" + name)], [whole(name)])
+        add(plan, "g", lambda e: e.affine_select(T[name][:], T.zer[:, 0:128], [[-1, 128]], Alu.not_equal, SCALES[name], 0, 1),
+            [("zer", 0, 128)], [whole(name)])
 
     def affine(queue, out, olo, src, lo, n, mul, plus):
         o, i = T[out][:, olo:olo + n], T[src][:, lo:lo + n]
@@ -159,13 +171,17 @@ def rank_program(g, core, T, topo):
         narrow(pos, tb)
 
     def scatter_s(w, pos, c, d):
-        add(plan, "s", lambda e: e.activation(T[w][:, 0:WW].indirect(T[pos][:, c:d]), T.num[:, 16 * c:16 * d], Act.Silu),
-            [whole(pos), ("num", 16 * c, 16 * d)], [whole(w)])
+        if c < d:
+            add(plan, "s", lambda e: e.activation(T[w][:, 0:WW].indirect(T[pos][:, c:d]), T.num[:, 16 * c:16 * d], Act.Silu),
+                [whole(pos), ("num", 16 * c, 16 * d)], [whole(w)])
 
     def scatter_v(w, pos, c, d):
-        add(plan, "v", lambda e: e.tensor_scalar(T[w][:, 0:WW].indirect(T[pos][:, c:d]), T.num[:, 0:16 * (d - c)],
-                                                 1.0, float(16 * c), Alu.mult, Alu.add),
-            [whole(pos), ("num", 0, 16 * (d - c))], [whole(w)])
+        n0 = C["N0"] // 16
+        for lo in range(c, d, 2 * n0):
+            hi = min(d, lo + 2 * n0)
+            add(plan, "v", lambda e, lo=lo, hi=hi: e.tensor_scalar(
+                T[w][:, 0:WW].indirect(T[pos][:, lo:hi]), T.num[:, 0:16 * (hi - lo)], 1.0, float(16 * lo), Alu.mult, Alu.add),
+                [whole(pos), ("num", 0, 16 * (hi - lo))], [whole(w)])
 
     def combine(ov, os_, osum, inv, lo, hi):
         add(plan, "v", lambda e: e.tensor_tensor(T[osum][:, lo:hi], T[ov][:, lo:hi], T[os_][:, lo:hi], Alu.add),
@@ -173,109 +189,142 @@ def rank_program(g, core, T, topo):
         add(plan, "v", lambda e: e.tensor_scalar(T[inv][:, lo:hi], T[osum][:, lo:hi], 0.25 - BASE, 0.0, Alu.add, Alu.max),
             [(osum, lo, hi)], [(inv, lo, hi)])
 
-    def scan_b(src):
+    def scan_b(src, op):
         add(plan, "v", lambda e: e.tensor_tensor_scan(T.Bn[:, S - 2::-1], T[src][:, S - 1:0:-1], T.zer[:, 0:S - 1], 0.0,
-                                                      Alu.add, Alu.max),
+                                                      Alu.add, op),
             [whole(src), whole("zer")], [("Bn", 0, S - 1)])
 
-    def scan_f(src):
+    def scan_f(src, op):
         add(plan, "v", lambda e: e.tensor_tensor_scan(T.Fn[:, 1:S], T[src][:, 0:S - 1], T.zer[:, 0:S - 1], 0.0,
-                                                      Alu.add, Alu.max),
+                                                      Alu.add, op),
             [whole(src), whole("zer")], [("Fn", 1, S)])
 
-    def below(out, src, inv, lo, hi):
-        off = T[inv][:, lo // 16:hi // 16]
-        add(plan, "s", lambda e: e.activation(T[out][:, lo:hi], T[src][:, 0:S].indirect(off), Act.Relu, bias=15.0, scale=-1.0),
-            [whole(src), (inv, lo // 16, hi // 16)], [(out, lo, hi)])
-
-    def capped(inv, lo, hi):
-        off = T[inv][:, lo // 16:hi // 16]
-        add(plan, "v", lambda e: e.tensor_scalar(T.FG[:, lo:hi], T.Fn[:, 0:S].indirect(off), 15.0, None, Alu.min),
-            [whole("Fn"), (inv, lo // 16, hi // 16)], [("FG", lo, hi)])
+    def capped(h, queue, which, inv, lo, hi, own=False):
+        src, out = which + "n", which + str(h)
+        o, win = T[out][:, lo:hi], T[src][:, 0:S].indirect(T[inv][:, lo // 16:hi // 16])
+        if queue == "s":
+            fn = lambda e: e.activation(o, win, Act.Relu, bias=15.0, scale=-1.0 if h == 1 else 1.0)
+        elif h == 1:
+            fn = lambda e: e.tensor_scalar(o, win, 15.0, -1.0, Alu.min, Alu.mult)
+        elif own:
+            fn = lambda e: e.tensor_scalar(o, win, -15.0, -1.0, Alu.max, Alu.mult)
+        else:
+            fn = lambda e: e.tensor_scalar(o, win, 15.0, 0.0, Alu.add, Alu.max)
+        add(plan, queue, fn, [whole(src), (inv, lo // 16, hi // 16)], [(out, lo, hi)])
 
     def matmul(bank, n, mat, src, lo, start, stop, group):
         add(plan, "t", lambda e: e.matmul(T[bank][:, 0:n], T[mat][:], T[src][:, lo:lo + n], start, stop),
             [whole(mat), (src, lo, lo + n)], [whole(bank)], group=group)
 
-    def send(h, k):
-        r = (q + k) % N
-        dst = T.cores[r]
+    def send(h, k, srcs, slo, land, dlo, n):
+        dst = T.cores[(q + k) % N]
         rid, pid = topo.addr(dst, core)
-        sbuf = "S%d" % h
+        outgoing[0] += len(topo.engines(core, dst))
+        sem, mask = T.sem["a%d_%d" % (h, k)], topo.mask(core, dst)
 
         def fn(e):
-            e.remote_dma(T["X%d" % h][:, q * HALF:(q + 1) * HALF], T[sbuf][:, r * HALF:(r + 1) * HALF],
-                         T.sem["a%d_%d" % (h, k)], T.sem.sent, pid, rid, topo.mask(core, dst))
-        add(plan, "g", fn, [(sbuf, r * HALF, (r + 1) * HALF)], [])
-
-    def exchange(h, inv, steps, extra=None):
-        steps = [(w[0], int(w[1])) for w in steps.split()]
-        by_s = [k for what, k in steps if what == "s"]
-        terms = {}
-
-        def term(k, mat, src, c):
-            i = terms.get(k, 0)
-            terms[k] = i + 1
-            matmul("Q%d" % k, HALF, mat, src, c, i == 0, i == 3, ("pack", h, k))
-        for what, k in steps:
-            r = (q + k) % N
-            lo, mid, hi = r * CAP, r * CAP + HALF, (r + 1) * CAP
-            if what in "bcd":
-                below("RB", "Bn", inv, mid if what == "d" else lo, mid if what == "c" else hi)
-                if what != "d":
-                    term(k, "un", "RB", lo)
-                if what != "c":
-                    term(k, "ln", "RB", mid)
-            elif what == "s":
-                below("FG", "Fn", inv, lo, mid)
-                term(k, "un", "FG", lo)
-            elif what == "u":
-                capped(inv, lo, mid)
-                term(k, "up", "FG", lo)
-            elif what == "l":
-                capped(inv, mid, hi)
-                term(k, "lp", "FG", mid)
-            elif what == "x":
-                extra()
+            if len(srcs) == 1:
+                e.remote_dma(T[land][:, dlo:dlo + n], T[srcs[0]][:, slo:slo + n], sem, T.sem.sent, pid, rid, mask)
             else:
-                affine("v", "S%d" % h, r * HALF, "Q%d" % k, 0, HALF, 1.0, 15.0 * 32 if k in by_s else 0.0)
-                send(h, k)
+                e.remote_dma_fused([RemoteDMATransfer(
+                    dst_ids=[DstId(rid=rid, pnc=pid)], dma_engine_mask=mask, remote_sem=sem,
+                    srcs=[T[s][:, slo:slo + n] for s in srcs], dsts=[T[land][:, dlo:dlo + n]], alu_op=1)],
+                    local_sem=T.sem.sent)
+        add(plan, "g", fn, [(s, slo, slo + n) for s in srcs], [])
 
-    def own(h, inv, by_tensor):
-        lo, hi, out = q * CAP, (q + 1) * CAP, "R%d" % h
-        below("RB", "Bn", inv, lo, hi)
-        capped(inv, lo, hi)
-        if not by_tensor:
-            add(plan, "v", lambda e: e.tensor_tensor(T[out][:, lo:hi], T.FG[:, lo:hi], T.RB[:, lo:hi], Alu.subtract),
-                [("FG", lo, hi), ("RB", lo, hi)], [(out, lo, hi)])
-            return
-        for k in range(2):
-            c, bank = lo + k * HALF, "Q%d" % (k + 1)
-            matmul(bank, HALF, "ln", "RB", c, True, False, ("own", h, k))
-            matmul(bank, HALF, "lp", "FG", c, False, True, ("own", h, k))
-            affine("s", out, c, bank, 0, HALF, 1.0, 0.0)
+    def parse(h):
+        out = []
+        for w in C["X%d" % h].split():
+            i = 2 if w[0] in "vs" else 1
+            out.append((w[:i], int(w[i]), PARTS[w[i + 1:]]))
+        return out
 
-    def unpack(h, helper):
+    def exchange(h, inv):
+        steps = parse(h)
+        packed = [k for what, k, _ in steps if what == "p"]
+        folded = [k for what, k, _ in steps if what == "f"]
+        summed = [(k, c) for what, k, (lo, hi) in steps if what == "d" for c in range(lo, hi, HALF)]
+        terms, by, bank = {}, {}, {}
+        for what, k, (lo, hi) in steps:
+            r = (q + k) % N
+            if what == "f":
+                send(h, k, ["F%d" % h, "B%d" % h], r * CAP + lo, "R1" if h == 1 else "D2", q * CAP + lo, hi - lo)
+            elif what == "p":
+                c, mid = r * HALF, r * CAP + HALF
+                add(plan, "v", lambda e, c=c, mid=mid, k=k: e.tensor_tensor(
+                    T["S%d" % h][:, c:c + HALF], T["Q%d" % k][:, 0:HALF], T["F%d" % h][:, mid:mid + HALF], Alu.add),
+                    [whole("Q%d" % k), ("F%d" % h, mid, mid + HALF)], [("S%d" % h, c, c + HALF)])
+                send(h, k, ["S%d" % h], c, "X%d" % h, q * HALF, HALF)
+            elif what == "c":
+                out, a, b = ("E%d" if k else "R%d") % h, r * CAP + lo, r * CAP + hi
+                add(plan, "v", lambda e, out=out, a=a, b=b: e.tensor_tensor(
+                    T[out][:, a:b], T["F%d" % h][:, a:b], T["B%d" % h][:, a:b], Alu.add if h == 1 else Alu.subtract),
+                    [("F%d" % h, a, b), ("B%d" % h, a, b)], [(out, a, b)])
+            elif what == "d":
+                out = ("E%d" if k else "R%d") % h
+                for c in range(lo, hi, HALF):
+                    both = by[("F", k, c)] == "s"
+                    affine("s", out, r * CAP + c, bank[(k, c)], 0, HALF, 1.0, 15.0 * (2 * h - 3) if both else 0.0)
+            elif what == "e":
+                send(h, k, ["E%d" % h], r * CAP + lo, "R%d" % h, q * CAP + lo, hi - lo)
+            elif what == "n":
+                narrow("ub", "lb") if h == 1 else narrow("ua", "la")
+            elif what == "r":
+                receive(h, [k])
+            else:
+                capped(h, what[0], what[1], inv, r * CAP + lo, r * CAP + hi, k not in folded)
+                for c in range(lo, hi, HALF):
+                    by[(what[1], k, c)] = what[0]
+                    if (k, c) in summed:
+                        first = (k, c) not in bank
+                        if first:
+                            bank[(k, c)] = "Q%d" % (len(bank) % 2 + (1 if packed else 2))
+                        mat = "lp" if h == 1 or what[0] == "v" else "ln"
+                        matmul(bank[(k, c)], HALF, mat, what[1] + str(h), r * CAP + c, first, not first, ("sum", h, k, c))
+                for c in range(lo, hi, HALF) if k in packed else ():
+                    if what[1] == "F" and c:
+                        continue
+                    i = terms.get(k, 0)
+                    terms[k] = i + 1
+                    mat = ("l" if c else "u") + ("p" if h == 1 or what[0] == "v" else "n")
+                    matmul("Q%d" % k, HALF, mat, what[1] + str(h), r * CAP + c, i == 0, i == 2, ("pack", h, k))
+
+    def receive(h, blocks=None):
         x, out = "X%d" % h, "R%d" % h
-        for k in range(1, N):
+        steps = parse(h)
+        for k in blocks or [k for k in range(1, N) if ("r", k, PARTS[""]) not in steps]:
             r = (q - k) % N
             c, lo = r * HALF, r * CAP
-            add(plan, None, None, [], [(x, c, c + HALF)], sem=("a%d_%d" % (h, k), len(topo.engines(T.cores[r], core))))
-            affine("v", "U", c, x, c, HALF, 1.0 / 32, MID)
-            affine("v", "V", c, "U", c, HALF, -32.0, 32 * MID)
-            affine(helper[k - 1], out, lo, "U", c, HALF, 1.0, -MID)
-            add(plan, "v", lambda e, c=c, lo=lo: e.tensor_tensor(T[out][:, lo + HALF:lo + CAP], T[x][:, c:c + HALF],
-                                                                 T.V[:, c:c + HALF], Alu.add),
-                [(x, c, c + HALF), ("V", c, c + HALF)], [(out, lo + HALF, lo + CAP)])
+            writes = sum(1 for what, kk, _ in steps if kk == k and what in "fpe")
+            sem = ("a%d_%d" % (h, k), writes * len(topo.engines(T.cores[r], core)))
+            if ("p", k, PARTS[""]) in steps:
+                add(plan, None, None, [], [(x, c, c + HALF)], sem=sem)
+                add(plan, "v", lambda e, c=c: e.tensor_scalar(T.U[:, c:c + HALF], T[x][:, c:c + HALF], ROUND, ROUND,
+                                                              Alu.add, Alu.subtract),
+                    [(x, c, c + HALF)], [("U", c, c + HALF)])
+                plus = 15.0 * (2 * h - 3) if ("sF", k, PARTS["a"]) in steps else 0.0
+                affine(C["TURN%d" % h][k - 1], out, lo, "U", c, HALF, 1.0 / 32, plus)
+                add(plan, "v", lambda e, c=c, lo=lo: e.tensor_tensor(T[out][:, lo + HALF:lo + CAP], T[x][:, c:c + HALF],
+                                                                     T.U[:, c:c + HALF], Alu.subtract),
+                    [(x, c, c + HALF), ("U", c, c + HALF)], [(out, lo + HALF, lo + CAP)])
+            elif h == 1 or not any(what == "f" and kk == k for what, kk, _ in steps):
+                add(plan, None, None, [], [(out, lo, lo + CAP)], sem=sem)
+            else:
+                add(plan, None, None, [], [("D2", lo, lo + CAP)], sem=sem)
+                if k < N - 1:
+                    affine("v", out, lo, "D2", lo, CAP, -1.0, 15.0)
+                else:
+                    affine("v", out, lo, "D2", lo, 416, -1.0, 15.0)
+                    affine("s", out, lo + 416, "D2", lo + 416, CAP - 416, -1.0, 15.0)
 
-    def channel_in(src, banks, nv):
+    def channel_in(src, mat, banks, nv):
         nc = (S - nv) // 2
         for k, p in enumerate(banks):
-            matmul(p, nc, "lp", src, nv + k * nc, True, False, p)
+            matmul(p, nc, mat, src, nv + k * nc, True, False, p)
 
-    def gather_v(out, rbuf, off, src, lo, hi):
+    def gather_v(out, rbuf, off, src, lo, hi, op):
         add(plan, "v", lambda e: e.tensor_tensor(T[out][:, lo:hi], T[rbuf][:, 0:SLOTS].indirect(T[off][:, lo // 16:hi // 16]),
-                                                 T[src][:, lo:hi], Alu.add),
+                                                 T[src][:, lo:hi], op),
             [whole(rbuf), whole(off), (src, lo, hi)], [(out, lo, hi)])
 
     def gather_s(out, rbuf, off, banks, nv):
@@ -294,21 +343,24 @@ def rank_program(g, core, T, topo):
     def store(queue, lo, hi):
         dma(queue, T.y[:, lo:hi], T.Y[:, lo:hi], [("Y", lo, hi)], [("y", lo, hi)])
 
+    n0, n1 = C["N0"], 16 * KA
     load("y", "la", T.sa)
-    numbers(0, 16 * KA)
+    numbers(0, n0)
     memset("Z", 0, WW // 16, 0.0)
     fill("s", "Was")
     fill("y", "Wav")
     load("y", "lb", T.sb)
     load("s", "A", T.a)
     add(plan, "s", lambda e: e.activation(T.Bn[:, S - 1:S], T.Z[:, 0:1], Act.Silu), [whole("Z")], [("Bn", S - 1, S)])
+    affine("s", "num", n0, "num", 0, n1 - n0, 1.0, float(n0))
     fill("y", "Wbs")
     memset("zer", 0, S, 0.0)
     memset("Fn", 0, 1, 0.0)
+    if 16 * KB1 > n1:
+        numbers(n1, 16 * KB1)
     for name in SCALES:
-        memset("c" + name, 0, 128, SCALES[name])
-        identity(name)
-    numbers(16 * KA, NI)
+        if packs or name[0] == "l":
+            identity(name)
 
     positions("la", "t1", "t2", "posa")
     scatter_s("Was", "posa", 0, KA)
@@ -319,42 +371,38 @@ def rank_program(g, core, T, topo):
     load("y", "B", T.b)
     fill("y", "Wbv")
     scatter_s("Wbs", "posb", 0, KB0)
-    channel_in("A", ["P2", "P3"], NV2)
-    scan_b("A")
-    scan_f("A")
-    narrow("ub", "lb")
-    first = (q + 1) % N
-    combine("Oav", "Oas", "Osa", "inva", first * KB, (first + 1) * KB)
-
-    def others():
-        for lo, hi in (((first + 1) * KB, N * KB), (0, first * KB)):
-            if lo < hi:
-                combine("Oav", "Oas", "Osa", "inva", lo, hi)
-    exchange(1, "inva", "u1 c1 l1 d1 x0 p1 u2 b2 l2 b3 l3 p2 s3 p3", others)
-    channel_in("B", ["P0", "P1"], NV1)
-    own(1, "inva", False)
+    channel_in("A", "lp", ["P2", "P3"], NV2)
+    scan_b("A", Alu.max)
+    scan_f("A", Alu.max)
+    combine("Oav", "Oas", "Osa", "inva", 0, N * KB)
+    exchange(1, "inva")
+    channel_in("B", "ln", ["P0", "P1"], NV1)
 
     scatter_s("Wbs", "posb", KB0, KB1)
     scatter_v("Wbv", "posb", KB1, 128)
     regroup("Wbv", "Obv")
     regroup("Wbs", "Obs")
 
-    unpack(1, "vvs")
-    gather_v("L", "R1", "ub", "B", 0, NV1)
+    receive(1)
+    gather_v("L", "R1", "ub", "B", 0, NV1, Alu.subtract)
     gather_s("L", "R1", "ub", ["P0", "P1"], NV1)
-    combine("Obv", "Obs", "Osb", "invb", 0, N * KB)
-    scan_b("L")
-    scan_f("L")
-    exchange(2, "invb", "b1 u1 b2 l1 s2 l2 p1 l3 b3 p2 s3 p3")
-    own(2, "invb", True)
-    narrow("ua", "la")
+    if C.get("CB", 0) == 0:
+        combine("Obv", "Obs", "Osb", "invb", 0, N * KB)
+    scan_b("L", Alu.min)
+    if C.get("CB", 0) == 1:
+        combine("Obv", "Obs", "Osb", "invb", 0, N * KB)
+    scan_f("L", Alu.min)
+    exchange(2, "invb")
 
-    unpack(2, "sss")
-    gather_v("Y", "R2", "ua", "A", 0, CUT)
-    gather_v("Y", "R2", "ua", "A", CUT, NV2)
+    receive(2)
+    cuts = [0] + list(C["CUTS"]) + [NV2]
+    for lo, hi in zip(cuts, cuts[1:]):
+        gather_v("Y", "R2", "ua", "A", lo, hi, Alu.add)
     gather_s("Y", "R2", "ua", ["P2", "P3"], NV2)
-    store("y", 0, CUT)
-    store("y", CUT, S)
+    mid = (NV2 + S) // 2
+    pieces = list(zip(cuts, cuts[1:]))
+    for lo, hi in pieces[:-1] + [(NV2, mid), pieces[-1], (mid, S)]:
+        store("y", lo, hi)
     add(plan, "y", None, [("y", 0, S)], [])
     emit(plan, queues, T)
-    g.wait_ge(T.sem.sent, 2 * outgoing)
+    g.wait_ge(T.sem.sent, outgoing[0])

@@ -1,58 +1,67 @@
 from concourse.mybir import AluOpType as Alu, ActivationFunctionType as Act
-from concourse.bass import DstId, RemoteDMATransfer
 
 N, S, CAP = 4, 2048, 576
 SLOTS = N * CAP
 HALF = CAP // 2
 KB = CAP // 16
-WW = 4096
+KW = SLOTS // 16
+UNIT = 32
 BASE = 32
-NI = 2048
-ROUND = 1.5 * 2.0 ** 28
-PARTS = {"": (0, CAP), "a": (0, HALF), "b": (HALF, CAP)}
+ROUND = 1.5 * 2.0 ** 23
+PARTS = {"": (0, 18), "a": (0, 9), "b": (9, 18)}
 CFG = {
     "KA": 70,
-    "KB0": 32, "KB1": 102,
-    "NV1": 1280, "NV2": 1280,
-    "N0": 704,
-    "CUTS": (512, 896),
-    "X1": "vF1a sB1a sB1b vF1b vF2a p1 sB2 vF2b sB3 vF3b p2 sF3a vF0a p3 sB0 vF0b c0 n0",
-    "X2": "sB1 vF1a vF1b p1 sB2 vF2a vF2b sF3a sB3 p2 vF3b p3 sB0 sF0 n0 r1 d0 r2",
-    "TURN1": "vvs", "TURN2": "vvs", "CB": 0,
+    "KB0": 32, "KB1": 88,
+    "N0": 800,
+    "L": (1152, 1280, 1664),
+    "Y": (512, 992, 1344, 1728),
+    "X1": "sB1:0:2 vF1:0:2 n0 c1:0:2 e1:0:2 vF1:2:10 sB1:2:18 sB2 sF2a vF1:10:18 vF2b p1:2:18 sB3 m0 p2 vG3 e3"
+          " vS0:0:14 sB0 i0 sS0 t1:2:18 t2 vS0:14:18 vG0",
+    "X2": "sB1 vF1a sB2 sF2a sB3a sB3b vF1b p1 vF2b vF3a p2 vF3b p3 sB0 sF0a sF0b n0 rv1 rv2 d0a d0b rs3",
 }
-SCALES = {"lp": 1.0, "ln": -1.0, "up": 32.0, "un": -32.0}
+SCALES = {"lp": 1.0, "ln": -1.0, "up": 32.0, "un": -32.0, "dp": 1.0 / 32}
 
 SCRATCH = {
     "A": ("sbuf", [128, S], "bfloat16"), "B": ("sbuf", [128, S], "bfloat16"),
     "la": ("sbuf", [128, 128], "int32"), "lb": ("sbuf", [128, 128], "int32"),
-    "t1": ("sbuf", [128, 128], "int32"), "t2": ("sbuf", [128, 128], "int32"),
-    "t3": ("sbuf", [128, 128], "int32"), "t4": ("sbuf", [128, 128], "int32"),
+    "ka": ("sbuf", [128, 128], "int32"), "kb": ("sbuf", [128, 128], "int32"),
+    "fa": ("sbuf", [128, 128], "float32"), "fb": ("sbuf", [128, 128], "float32"),
+    "da": ("sbuf", [128, 128], "float32"), "db": ("sbuf", [128, 128], "float32"),
     "posa": ("sbuf", [128, 128], "uint16"), "posb": ("sbuf", [128, 128], "uint16"),
     "ua": ("sbuf", [128, 128], "uint16"), "ub": ("sbuf", [128, 128], "uint16"),
-    "Z": ("sbuf", [128, WW // 16], "float32"), "zer": ("sbuf", [128, S], "bfloat16"),
-    "num": ("sbuf", [128, NI], "float32"),
-    "Wav": ("sbuf", [128, WW], "float32"), "Was": ("sbuf", [128, WW], "float32"),
-    "Wbv": ("sbuf", [128, WW], "float32"), "Wbs": ("sbuf", [128, WW], "float32"),
-    "Oav": ("sbuf", [128, WW // 16], "float32"), "Oas": ("sbuf", [128, WW // 16], "float32"),
-    "Obv": ("sbuf", [128, WW // 16], "float32"), "Obs": ("sbuf", [128, WW // 16], "float32"),
-    "Osa": ("sbuf", [128, N * KB], "float32"), "Osb": ("sbuf", [128, N * KB], "float32"),
-    "inva": ("sbuf", [128, N * KB], "uint16"), "invb": ("sbuf", [128, N * KB], "uint16"),
-    "Fn": ("sbuf", [128, S], "bfloat16"), "Bn": ("sbuf", [128, S], "bfloat16"),
+    "Z": ("sbuf", [128, KW], "float32"), "zer": ("sbuf", [128, S], "bfloat16"),
+    "num": ("sbuf", [128, S], "float32"),
+    "Wv": ("sbuf", [128, SLOTS], "float32"),
+    "Was": ("sbuf", [128, SLOTS], "float32"), "Wbs": ("sbuf", [128, SLOTS], "float32"),
+    "Oav": ("sbuf", [128, KW], "float32"), "Oas": ("sbuf", [128, KW], "float32"),
+    "Obv": ("sbuf", [128, KW], "float32"), "Obs": ("sbuf", [128, KW], "float32"),
+    "Oa": ("sbuf", [128, KW], "float32"), "Ob": ("sbuf", [128, KW], "float32"),
+    "inva": ("sbuf", [128, KW], "uint16"), "invb": ("sbuf", [128, KW], "uint16"),
+    "Fn": ("sbuf", [128, S], "bfloat16"), "Fm": ("sbuf", [128, S], "bfloat16"), "Bn": ("sbuf", [128, S], "bfloat16"),
     "F1": ("sbuf", [128, SLOTS], "bfloat16"), "B1": ("sbuf", [128, SLOTS], "bfloat16"),
     "F2": ("sbuf", [128, SLOTS], "bfloat16"), "B2": ("sbuf", [128, SLOTS], "bfloat16"),
     "S1": ("sbuf", [128, N * HALF], "float16"), "S2": ("sbuf", [128, N * HALF], "float16"),
     "X1": ("sbuf", [128, N * HALF], "float16"), "X2": ("sbuf", [128, N * HALF], "float16"),
-    "E1": ("sbuf", [128, SLOTS], "bfloat16"), "E2": ("sbuf", [128, SLOTS], "bfloat16"),
-    "U": ("sbuf", [128, N * HALF], "bfloat16"), "D2": ("sbuf", [128, SLOTS], "bfloat16"),
+    "E": ("sbuf", [128, SLOTS], "bfloat16"), "U": ("sbuf", [128, N * HALF], "bfloat16"),
     "R1": ("sbuf", [128, SLOTS], "bfloat16"), "R2": ("sbuf", [128, SLOTS], "bfloat16"),
     "L": ("sbuf", [128, S], "bfloat16"), "Y": ("sbuf", [128, S], "bfloat16"),
     "G": ("sbuf", [128, 1024], "bfloat16"),
 }
 for _n in SCALES:
     SCRATCH[_n] = ("sbuf", [128, 128], "bfloat16")
-for _n in ("P0", "P1", "P2", "P3", "Q1", "Q2", "Q3"):
+for _n in ("P0", "P1", "P2", "P3", "Q0", "Q1", "Q2", "Q3"):
     SCRATCH[_n] = ("psum", [128, 512], "float32")
-SEMAPHORES = ["sent"] + ["a%d_%d" % (h, k) for h in (1, 2) for k in range(1, N)] + ["e%d" % i for i in range(140)]
+SEMAPHORES = ["sent"] + ["a%d_%d" % (h, k) for h in (1, 2) for k in range(5)] + ["e%d" % i for i in range(139)]
+
+
+def parse(text):
+    out = []
+    for w in text.split():
+        i = min(j for j, ch in enumerate(w) if ch.isdigit())
+        rest = w[i + 1:]
+        lo, hi = PARTS[rest] if rest in PARTS else [int(v) for v in rest.split(":")[1:]]
+        out.append((w[:i], int(w[i]), lo * UNIT, hi * UNIT))
+    return out
 
 
 def new_plan():
@@ -121,11 +130,10 @@ def rank_program(g, core, T, topo):
     if q is None:
         return
     C = CFG
-    KA, KB0, KB1, NV1, NV2 = C["KA"], C["KB0"], C["KB1"], C["NV1"], C["NV2"]
+    KA, KB0, KB1 = C["KA"], C["KB0"], C["KB1"]
     plan = new_plan()
     queues = {"g": g, "v": g.vector, "s": g.scalar, "y": g.sync, "t": g.tensor}
     outgoing = [0]
-    packs = "p" in C["X1"] + C["X2"]
 
     def whole(name):
         return (name, 0, T[name].shape[1])
@@ -133,8 +141,8 @@ def rank_program(g, core, T, topo):
     def dma(queue, out, in_, reads, writes):
         add(plan, queue, lambda e: e.dma_start(out, in_), reads, writes, inc=16)
 
-    def load(queue, dst, src):
-        dma(queue, T[dst][:], src[:], [], [whole(dst)])
+    def load(dst, src):
+        dma("y", T[dst][:], src[:], [], [whole(dst)])
 
     def fill(queue, w):
         dma(queue, T[w][0:128:16, :], T.Z[:], [whole("Z")], [whole(w)])
@@ -153,256 +161,228 @@ def rank_program(g, core, T, topo):
         add(plan, "g", lambda e: e.affine_select(T[name][:], T.zer[:, 0:128], [[-1, 128]], Alu.not_equal, SCALES[name], 0, 1),
             [("zer", 0, 128)], [whole(name)])
 
+    def scalar(out, olo, src, lo, n, s1, s2, *ops):
+        add(plan, "v", lambda e: e.tensor_scalar(T[out][:, olo:olo + n], T[src][:, lo:lo + n], s1, s2, *ops),
+            [(src, lo, lo + n)], [(out, olo, olo + n)])
+
     def affine(queue, out, olo, src, lo, n, mul, plus):
-        o, i = T[out][:, olo:olo + n], T[src][:, lo:lo + n]
         if queue == "v":
-            fn = lambda e: e.tensor_scalar(o, i, mul, plus, Alu.mult, Alu.add)
+            scalar(out, olo, src, lo, n, mul, plus, Alu.mult, Alu.add)
         else:
-            fn = lambda e: e.activation(o, i, Act.Identity, bias=plus, scale=mul)
-        add(plan, queue, fn, [(src, lo, lo + n)], [(out, olo, olo + n)])
+            add(plan, "s", lambda e: e.activation(T[out][:, olo:olo + n], T[src][:, lo:lo + n], Act.Identity,
+                                                  bias=plus, scale=mul), [(src, lo, lo + n)], [(out, olo, olo + n)])
+
+    def both(out, olo, a, alo, b, blo, n, op):
+        add(plan, "v", lambda e: e.tensor_tensor(T[out][:, olo:olo + n], T[a][:, alo:alo + n], T[b][:, blo:blo + n], op),
+            [(a, alo, alo + n), (b, blo, blo + n)], [(out, olo, olo + n)])
 
     def narrow(out, src):
         add(plan, "v", lambda e: e.tensor_copy(T[out][:], T[src][:]), [whole(src)], [whole(out)])
 
-    def positions(lst, ta, tb, pos):
-        add(plan, "v", lambda e: e.tensor_scalar(T[ta][:], T[lst][:], WW + 1, None, Alu.mult), [whole(lst)], [whole(ta)])
-        add(plan, "v", lambda e: e.tensor_scalar(T[tb][:], T[ta][:], 4, WW - 1, Alu.logical_shift_right, Alu.bitwise_and),
-            [whole(ta)], [whole(tb)])
-        narrow(pos, tb)
+    def position(x, step):
+        if step == 0:
+            scalar("k" + x, 0, "l" + x, 0, 128, 4, None, Alu.logical_shift_right)
+        elif step == 1:
+            scalar("f" + x, 0, "l" + x, 0, 128, KW / (SLOTS - 1.0), None, Alu.mult)
+        elif step == 2:
+            both("d" + x, 0, "f" + x, 0, "k" + x, 0, 128, Alu.subtract)
+        else:
+            affine("v", "pos" + x, 0, "d" + x, 0, 128, SLOTS - 1.0, 0.25)
 
     def scatter_s(w, pos, c, d):
-        if c < d:
-            add(plan, "s", lambda e: e.activation(T[w][:, 0:WW].indirect(T[pos][:, c:d]), T.num[:, 16 * c:16 * d], Act.Silu),
-                [whole(pos), ("num", 16 * c, 16 * d)], [whole(w)])
+        add(plan, "s", lambda e: e.activation(T[w][:].indirect(T[pos][:, c:d]), T.num[:, 16 * c:16 * d], Act.Silu),
+            [whole(pos), ("num", 16 * c, 16 * d)], [whole(w)])
 
-    def scatter_v(w, pos, c, d):
-        n0 = C["N0"] // 16
-        for lo in range(c, d, 2 * n0):
-            hi = min(d, lo + 2 * n0)
-            add(plan, "v", lambda e, lo=lo, hi=hi: e.tensor_scalar(
-                T[w][:, 0:WW].indirect(T[pos][:, lo:hi]), T.num[:, 0:16 * (hi - lo)], 1.0, float(16 * lo), Alu.mult, Alu.add),
-                [whole(pos), ("num", 0, 16 * (hi - lo))], [whole(w)])
+    def scatter_v(pos, c, d, sign):
+        add(plan, "v", lambda e: e.tensor_scalar(T.Wv[:].indirect(T[pos][:, c:d]), T.num[:, 0:16 * (d - c)],
+                                                 sign, sign * 16 * c, Alu.mult, Alu.add),
+            [whole(pos), ("num", 0, 16 * (d - c))], [whole("Wv")])
 
-    def combine(ov, os_, osum, inv, lo, hi):
-        add(plan, "v", lambda e: e.tensor_tensor(T[osum][:, lo:hi], T[ov][:, lo:hi], T[os_][:, lo:hi], Alu.add),
-            [whole(ov), whole(os_)], [(osum, lo, hi)])
-        add(plan, "v", lambda e: e.tensor_scalar(T[inv][:, lo:hi], T[osum][:, lo:hi], 0.25 - BASE, 0.0, Alu.add, Alu.max),
-            [(osum, lo, hi)], [(inv, lo, hi)])
+    def offsets(inv, src, lo, n):
+        scalar(inv, lo, src, lo, n, 0.25 - BASE, 0.0, Alu.add, Alu.max)
 
-    def scan_b(src, op):
+    def scans(src, op):
         add(plan, "v", lambda e: e.tensor_tensor_scan(T.Bn[:, S - 2::-1], T[src][:, S - 1:0:-1], T.zer[:, 0:S - 1], 0.0,
-                                                      Alu.add, op),
-            [whole(src), whole("zer")], [("Bn", 0, S - 1)])
-
-    def scan_f(src, op):
+                                                      Alu.add, op), [whole(src), whole("zer")], [("Bn", 0, S - 1)])
         add(plan, "v", lambda e: e.tensor_tensor_scan(T.Fn[:, 1:S], T[src][:, 0:S - 1], T.zer[:, 0:S - 1], 0.0,
-                                                      Alu.add, op),
-            [whole(src), whole("zer")], [("Fn", 1, S)])
+                                                      Alu.add, op), [whole(src), whole("zer")], [("Fn", 1, S)])
 
-    def capped(h, queue, which, inv, lo, hi, own=False):
+    def capped(h, queue, which, inv, lo, hi, scale):
         src, out = which + "n", which + str(h)
         o, win = T[out][:, lo:hi], T[src][:, 0:S].indirect(T[inv][:, lo // 16:hi // 16])
         if queue == "s":
             fn = lambda e: e.activation(o, win, Act.Relu, bias=15.0, scale=-1.0 if h == 1 else 1.0)
         elif h == 1:
-            fn = lambda e: e.tensor_scalar(o, win, 15.0, -1.0, Alu.min, Alu.mult)
-        elif own:
-            fn = lambda e: e.tensor_scalar(o, win, -15.0, -1.0, Alu.max, Alu.mult)
+            fn = lambda e: e.tensor_scalar(o, win, 15.0, -scale, Alu.min, Alu.mult)
         else:
-            fn = lambda e: e.tensor_scalar(o, win, 15.0, 0.0, Alu.add, Alu.max)
+            fn = lambda e: e.tensor_scalar(o, win, -15.0, -scale, Alu.max, Alu.mult)
         add(plan, queue, fn, [whole(src), (inv, lo // 16, hi // 16)], [(out, lo, hi)])
+
+    def gathered(out, win, off, other, lo, hi, op):
+        add(plan, "v", lambda e: e.tensor_tensor(T[out][:, lo:hi], T[win][:].indirect(T[off][:, lo // 16:hi // 16]),
+                                                 T[other][:, lo:hi], op),
+            [whole(win), (off, lo // 16, hi // 16), (other, lo, hi)], [(out, lo, hi)])
 
     def matmul(bank, n, mat, src, lo, start, stop, group):
         add(plan, "t", lambda e: e.matmul(T[bank][:, 0:n], T[mat][:], T[src][:, lo:lo + n], start, stop),
             [whole(mat), (src, lo, lo + n)], [whole(bank)], group=group)
 
-    def send(h, k, srcs, slo, land, dlo, n):
+    def send(k, sem, src, slo, land, dlo, n):
         dst = T.cores[(q + k) % N]
         rid, pid = topo.addr(dst, core)
         outgoing[0] += len(topo.engines(core, dst))
-        sem, mask = T.sem["a%d_%d" % (h, k)], topo.mask(core, dst)
+        add(plan, "g", lambda e: e.remote_dma(T[land][:, dlo:dlo + n], T[src][:, slo:slo + n], T.sem[sem], T.sem.sent,
+                                              pid, rid, topo.mask(core, dst)), [(src, slo, slo + n)], [])
 
-        def fn(e):
-            if len(srcs) == 1:
-                e.remote_dma(T[land][:, dlo:dlo + n], T[srcs[0]][:, slo:slo + n], sem, T.sem.sent, pid, rid, mask)
-            else:
-                e.remote_dma_fused([RemoteDMATransfer(
-                    dst_ids=[DstId(rid=rid, pnc=pid)], dma_engine_mask=mask, remote_sem=sem,
-                    srcs=[T[s][:, slo:slo + n] for s in srcs], dsts=[T[land][:, dlo:dlo + n]], alu_op=1)],
-                    local_sem=T.sem.sent)
-        add(plan, "g", fn, [(s, slo, slo + n) for s in srcs], [])
-
-    def parse(h):
-        out = []
-        for w in C["X%d" % h].split():
-            i = 2 if w[0] in "vs" else 1
-            out.append((w[:i], int(w[i]), PARTS[w[i + 1:]]))
-        return out
-
-    def exchange(h, inv):
-        steps = parse(h)
-        packed = [k for what, k, _ in steps if what == "p"]
-        folded = [k for what, k, _ in steps if what == "f"]
-        summed = [(k, c) for what, k, (lo, hi) in steps if what == "d" for c in range(lo, hi, HALF)]
-        terms, by, bank = {}, {}, {}
-        for what, k, (lo, hi) in steps:
-            r = (q + k) % N
-            if what == "f":
-                send(h, k, ["F%d" % h, "B%d" % h], r * CAP + lo, "R1" if h == 1 else "D2", q * CAP + lo, hi - lo)
-            elif what == "p":
-                c, mid = r * HALF, r * CAP + HALF
-                add(plan, "v", lambda e, c=c, mid=mid, k=k: e.tensor_tensor(
-                    T["S%d" % h][:, c:c + HALF], T["Q%d" % k][:, 0:HALF], T["F%d" % h][:, mid:mid + HALF], Alu.add),
-                    [whole("Q%d" % k), ("F%d" % h, mid, mid + HALF)], [("S%d" % h, c, c + HALF)])
-                send(h, k, ["S%d" % h], c, "X%d" % h, q * HALF, HALF)
-            elif what == "c":
-                out, a, b = ("E%d" if k else "R%d") % h, r * CAP + lo, r * CAP + hi
-                add(plan, "v", lambda e, out=out, a=a, b=b: e.tensor_tensor(
-                    T[out][:, a:b], T["F%d" % h][:, a:b], T["B%d" % h][:, a:b], Alu.add if h == 1 else Alu.subtract),
-                    [("F%d" % h, a, b), ("B%d" % h, a, b)], [(out, a, b)])
+    def exchange(h, inv, extra):
+        steps = parse(C["X%d" % h])
+        f, b, sbuf, x, out = ("%s%d" % (n, h) for n in "FBSXR")
+        carried = 15.0 * (2 * h - 3)
+        sends = [(k, lo, hi) for what, k, lo, hi in steps if what in "pe"]
+        fine = [(k, lo, hi) for what, k, lo, hi in steps if what == "t"]
+        pending, by, bank, arrived, turn = [], {}, {}, [], [0]
+        for what, k, lo, hi in steps:
+            mid = (lo + hi) // 2
+            if what == "p":
+                up, low = ("l", "d") if (k, lo, hi) in fine else ("u", "l")
+                pending += [((k, lo, hi), "F", lo, mid, up), ((k, lo, hi), "B", lo, mid, up), ((k, lo, hi), "B", mid, hi, low)]
             elif what == "d":
-                out = ("E%d" if k else "R%d") % h
-                for c in range(lo, hi, HALF):
-                    both = by[("F", k, c)] == "s"
-                    affine("s", out, r * CAP + c, bank[(k, c)], 0, HALF, 1.0, 15.0 * (2 * h - 3) if both else 0.0)
+                pending += [((k, lo, hi), "F", lo, hi, "l"), ((k, lo, hi), "B", lo, hi, "l")]
+
+        def next_bank():
+            turn[0] += 1
+            return "Q%d" % (turn[0] % N)
+
+        def arrive(k, lo, hi, buf, c, n):
+            arrived.append((k, lo, hi))
+            count = len(topo.engines(T.cores[(q - k) % N], core))
+            add(plan, None, None, [], [(buf, c, c + n)], sem=("a%d_%d" % (h, sends.index((k, lo, hi))), count))
+
+        for what, k, lo, hi in steps:
+            piece, mid, n = (k, lo, hi), (lo + hi) // 2, (hi - lo) // 2
+            to, fro = (q + k) % N * CAP, (q - k) % N * CAP
+            made = "E" if k else out
+            if what in extra:
+                extra[what](lo, hi)
+            elif what == "p":
+                both(sbuf, (to + lo) // 2, bank[piece], 0, f, to + mid, n, Alu.add)
+                send(k, "a%d_%d" % (h, sends.index(piece)), sbuf, (to + lo) // 2, x, (q * CAP + lo) // 2, n)
             elif what == "e":
-                send(h, k, ["E%d" % h], r * CAP + lo, "R%d" % h, q * CAP + lo, hi - lo)
-            elif what == "n":
-                narrow("ub", "lb") if h == 1 else narrow("ua", "la")
-            elif what == "r":
-                receive(h, [k])
-            else:
-                capped(h, what[0], what[1], inv, r * CAP + lo, r * CAP + hi, k not in folded)
-                for c in range(lo, hi, HALF):
-                    by[(what[1], k, c)] = what[0]
-                    if (k, c) in summed:
-                        first = (k, c) not in bank
-                        if first:
-                            bank[(k, c)] = "Q%d" % (len(bank) % 2 + (1 if packed else 2))
-                        mat = "lp" if h == 1 or what[0] == "v" else "ln"
-                        matmul(bank[(k, c)], HALF, mat, what[1] + str(h), r * CAP + c, first, not first, ("sum", h, k, c))
-                for c in range(lo, hi, HALF) if k in packed else ():
-                    if what[1] == "F" and c:
-                        continue
-                    i = terms.get(k, 0)
-                    terms[k] = i + 1
-                    mat = ("l" if c else "u") + ("p" if h == 1 or what[0] == "v" else "n")
-                    matmul("Q%d" % k, HALF, mat, what[1] + str(h), r * CAP + c, i == 0, i == 2, ("pack", h, k))
-
-    def receive(h, blocks=None):
-        x, out = "X%d" % h, "R%d" % h
-        steps = parse(h)
-        for k in blocks or [k for k in range(1, N) if ("r", k, PARTS[""]) not in steps]:
-            r = (q - k) % N
-            c, lo = r * HALF, r * CAP
-            writes = sum(1 for what, kk, _ in steps if kk == k and what in "fpe")
-            sem = ("a%d_%d" % (h, k), writes * len(topo.engines(T.cores[r], core)))
-            if ("p", k, PARTS[""]) in steps:
-                add(plan, None, None, [], [(x, c, c + HALF)], sem=sem)
-                add(plan, "v", lambda e, c=c: e.tensor_scalar(T.U[:, c:c + HALF], T[x][:, c:c + HALF], ROUND, ROUND,
-                                                              Alu.add, Alu.subtract),
-                    [(x, c, c + HALF)], [("U", c, c + HALF)])
-                plus = 15.0 * (2 * h - 3) if ("sF", k, PARTS["a"]) in steps else 0.0
-                affine(C["TURN%d" % h][k - 1], out, lo, "U", c, HALF, 1.0 / 32, plus)
-                add(plan, "v", lambda e, c=c, lo=lo: e.tensor_tensor(T[out][:, lo + HALF:lo + CAP], T[x][:, c:c + HALF],
-                                                                     T.U[:, c:c + HALF], Alu.subtract),
-                    [(x, c, c + HALF), ("U", c, c + HALF)], [(out, lo + HALF, lo + CAP)])
-            elif h == 1 or not any(what == "f" and kk == k for what, kk, _ in steps):
-                add(plan, None, None, [], [(out, lo, lo + CAP)], sem=sem)
-            else:
-                add(plan, None, None, [], [("D2", lo, lo + CAP)], sem=sem)
-                if k < N - 1:
-                    affine("v", out, lo, "D2", lo, CAP, -1.0, 15.0)
+                send(k, "a%d_%d" % (h, sends.index(piece)), "E", to + lo, out, q * CAP + lo, hi - lo)
+            elif what == "c":
+                both(made, to + lo, f, to + lo, b, to + lo, hi - lo, Alu.add)
+            elif what == "d":
+                affine("s", made, to + lo, bank[piece], 0, hi - lo, 1.0, carried if by[("F", k, lo)] == "s" else 0.0)
+            elif what == "m":
+                scalar("Fm", 0, "Fn", 0, S, 15.0, -1.0, Alu.min, Alu.mult)
+            elif what == "vG":
+                gathered(made, "Fm", inv, b, to + lo, to + hi, Alu.add)
+            elif what[0] in "rt":
+                c, a, lack = (fro + lo) // 2, fro + lo, carried if by[("F", k, lo)] == "s" else 0.0
+                arrive(k, lo, hi, x, c, n)
+                if what[0] == "r":
+                    scalar("U", c, x, c, n, 32 * ROUND, 32 * ROUND, Alu.add, Alu.subtract)
+                    affine(what[1], out, a, "U", c, n, 1.0 / 32, lack)
+                    both(out, fro + mid, x, c, "U", c, n, Alu.subtract)
                 else:
-                    affine("v", out, lo, "D2", lo, 416, -1.0, 15.0)
-                    affine("s", out, lo + 416, "D2", lo + 416, CAP - 416, -1.0, 15.0)
+                    p = next_bank()
+                    matmul(p, n, "up", x, c, True, False, ("split", h, piece))
+                    scalar(out, a, x, c, n, ROUND, ROUND - lack, Alu.add, Alu.subtract)
+                    matmul(p, n, "un", out, a, False, True, ("split", h, piece))
+                    affine("s", out, fro + mid, p, 0, n, 1.0, 32 * lack)
+            else:
+                small = what == "vF" and any(kk == k and (a + z) // 2 <= lo and hi <= z for kk, a, z in fine)
+                capped(h, what[0], what[1], inv, to + lo, to + hi, 1.0 / 32 if small else 1.0)
+                for c in range(lo, hi, UNIT):
+                    by[(what[1], k, c)] = what[0]
+                for term in list(pending):
+                    pc, which, a, z, weight = term
+                    if all((which, pc[0], c) in by for c in range(a, z, UNIT)):
+                        pending.remove(term)
+                        first = pc not in bank
+                        if first:
+                            bank[pc] = next_bank()
+                        sign = "p" if h == 1 or by[(which, pc[0], a)] == "v" else "n"
+                        matmul(bank[pc], z - a, weight + sign, which + str(h), (q + pc[0]) % N * CAP + a, first,
+                               not any(t[0] == pc for t in pending), ("sum", h, pc))
+        for k, lo, hi in sends:
+            if (k, lo, hi) not in arrived:
+                arrive(k, lo, hi, out, (q - k) % N * CAP + lo, hi - lo)
 
-    def channel_in(src, mat, banks, nv):
-        nc = (S - nv) // 2
-        for k, p in enumerate(banks):
-            matmul(p, nc, mat, src, nv + k * nc, True, False, p)
+    def channel_in(src, mat, banks, cuts):
+        for p, lo, hi in zip(banks, cuts, cuts[1:]):
+            matmul(p, hi - lo, mat, src, lo, True, False, p)
 
-    def gather_v(out, rbuf, off, src, lo, hi, op):
-        add(plan, "v", lambda e: e.tensor_tensor(T[out][:, lo:hi], T[rbuf][:, 0:SLOTS].indirect(T[off][:, lo // 16:hi // 16]),
-                                                 T[src][:, lo:hi], op),
-            [whole(rbuf), whole(off), (src, lo, hi)], [(out, lo, hi)])
-
-    def gather_s(out, rbuf, off, banks, nv):
-        nc = (S - nv) // 2
-        for k, p in enumerate(banks):
-            lo = nv + k * nc
-            add(plan, "s", lambda e, k=k, lo=lo: e.activation(
-                T.G[:, k * nc:(k + 1) * nc], T[rbuf][:, 0:SLOTS].indirect(T[off][:, lo // 16:(lo + nc) // 16]), Act.Copy),
-                [whole(rbuf), whole(off)], [("G", k * nc, (k + 1) * nc)])
-            matmul(p, nc, "lp", "G", k * nc, False, True, p)
-        for k, p in enumerate(banks):
-            lo = nv + k * nc
-            add(plan, "s", lambda e, p=p, lo=lo: e.activation(T[out][:, lo:lo + nc], T[p][:, 0:nc], Act.Copy),
-                [whole(p)], [(out, lo, lo + nc)])
-
-    def store(queue, lo, hi):
-        dma(queue, T.y[:, lo:hi], T.Y[:, lo:hi], [("Y", lo, hi)], [("y", lo, hi)])
+    def gather_s(out, rbuf, off, banks, cuts):
+        for p, lo, hi in zip(banks, cuts, cuts[1:]):
+            c = lo - cuts[0]
+            add(plan, "s", lambda e, c=c, lo=lo, hi=hi: e.activation(
+                T.G[:, c:c + hi - lo], T[rbuf][:].indirect(T[off][:, lo // 16:hi // 16]), Act.Copy),
+                [whole(rbuf), whole(off)], [("G", c, c + hi - lo)])
+            matmul(p, hi - lo, "lp", "G", c, False, True, p)
+        for p, lo, hi in zip(banks, cuts, cuts[1:]):
+            affine("s", out, lo, p, 0, hi - lo, 1.0, 0.0)
 
     n0, n1 = C["N0"], 16 * KA
-    load("y", "la", T.sa)
+    lcut, ycut = list(C["L"]) + [S], [0] + list(C["Y"]) + [S]
+    load("la", T.sa)
+    load("lb", T.sb)
     numbers(0, n0)
-    memset("Z", 0, WW // 16, 0.0)
+    memset("Z", 0, KW, 0.0)
     fill("s", "Was")
-    fill("y", "Wav")
-    load("y", "lb", T.sb)
-    load("s", "A", T.a)
+    fill("y", "Wv")
     add(plan, "s", lambda e: e.activation(T.Bn[:, S - 1:S], T.Z[:, 0:1], Act.Silu), [whole("Z")], [("Bn", S - 1, S)])
+    load("A", T.a)
     affine("s", "num", n0, "num", 0, n1 - n0, 1.0, float(n0))
     fill("y", "Wbs")
     memset("zer", 0, S, 0.0)
     memset("Fn", 0, 1, 0.0)
-    if 16 * KB1 > n1:
-        numbers(n1, 16 * KB1)
+    numbers(n1, 16 * KB1)
     for name in SCALES:
-        if packs or name[0] == "l":
-            identity(name)
+        identity(name)
 
-    positions("la", "t1", "t2", "posa")
+    for x, step in (("a", 0), ("a", 1), ("b", 0), ("a", 2), ("b", 1), ("a", 3), ("b", 2)):
+        position(x, step)
     scatter_s("Was", "posa", 0, KA)
-    scatter_v("Wav", "posa", KA, 128)
-    positions("lb", "t3", "t4", "posb")
-    regroup("Wav", "Oav")
+    scatter_v("posa", KA, 128, -1.0)
+    position("b", 3)
+    regroup("Wv", "Oav")
     regroup("Was", "Oas")
-    load("y", "B", T.b)
-    fill("y", "Wbv")
+    load("B", T.b)
     scatter_s("Wbs", "posb", 0, KB0)
-    channel_in("A", "lp", ["P2", "P3"], NV2)
-    scan_b("A", Alu.max)
-    scan_f("A", Alu.max)
-    combine("Oav", "Oas", "Osa", "inva", 0, N * KB)
-    exchange(1, "inva")
-    channel_in("B", "ln", ["P0", "P1"], NV1)
+    channel_in("A", "lp", ["P2", "P3"], ycut[-3:])
+    scans("A", Alu.max)
+    halves = [0, KW // 2] if (q + 1) % N < N // 2 else [KW // 2, 0]
+    for lo in halves:
+        both("Oa", lo, "Oas", lo, "Oav", lo, KW // 2, Alu.subtract)
+    for lo in halves:
+        offsets("inva", "Oa", lo, KW // 2)
 
-    scatter_s("Wbs", "posb", KB0, KB1)
-    scatter_v("Wbv", "posb", KB1, 128)
-    regroup("Wbv", "Obv")
-    regroup("Wbs", "Obs")
+    def rest_s(lo, hi):
+        scatter_s("Wbs", "posb", KB0, KB1)
+        regroup("Wbs", "Obs")
 
-    receive(1)
-    gather_v("L", "R1", "ub", "B", 0, NV1, Alu.subtract)
-    gather_s("L", "R1", "ub", ["P0", "P1"], NV1)
-    if C.get("CB", 0) == 0:
-        combine("Obv", "Obs", "Osb", "invb", 0, N * KB)
-    scan_b("L", Alu.min)
-    if C.get("CB", 0) == 1:
-        combine("Obv", "Obs", "Osb", "invb", 0, N * KB)
-    scan_f("L", Alu.min)
-    exchange(2, "invb")
+    def rest_v(lo, hi):
+        c, d = (KB1 + (128 - KB1) * v // CAP // 2 * 2 for v in (lo, hi))
+        scatter_v("posb", c, d, 1.0)
+        if hi == CAP:
+            regroup("Wv", "Obv")
+    exchange(1, "inva", {"n": lambda lo, hi: narrow("ub", "lb"), "sS": rest_s, "vS": rest_v,
+                         "i": lambda lo, hi: channel_in("B", "ln", ["P0", "P1"], lcut[-3:])})
 
-    receive(2)
-    cuts = [0] + list(C["CUTS"]) + [NV2]
-    for lo, hi in zip(cuts, cuts[1:]):
-        gather_v("Y", "R2", "ua", "A", lo, hi, Alu.add)
-    gather_s("Y", "R2", "ua", ["P2", "P3"], NV2)
-    mid = (NV2 + S) // 2
-    pieces = list(zip(cuts, cuts[1:]))
-    for lo, hi in pieces[:-1] + [(NV2, mid), pieces[-1], (mid, S)]:
-        store("y", lo, hi)
+    gathered("L", "R1", "ub", "B", 0, lcut[0], Alu.subtract)
+    gather_s("L", "R1", "ub", ["P0", "P1"], lcut[-3:])
+    both("Ob", 0, "Obs", 0, "Obv", 0, KW, Alu.max)
+    gathered("L", "R1", "ub", "B", lcut[0], lcut[1], Alu.subtract)
+    offsets("invb", "Ob", 0, KW)
+    scans("L", Alu.min)
+    exchange(2, "invb", {"n": lambda lo, hi: narrow("ua", "la")})
+
+    for lo, hi in zip(ycut[:3], ycut[1:4]):
+        gathered("Y", "R2", "ua", "A", lo, hi, Alu.add)
+    gather_s("Y", "R2", "ua", ["P2", "P3"], ycut[-3:])
+    for lo, hi in ((0, ycut[1]), (ycut[1], ycut[2]), (ycut[2], S)):
+        dma("y", T.y[:, lo:hi], T.Y[:, lo:hi], [("Y", lo, hi)], [("y", lo, hi)])
     add(plan, "y", None, [("y", 0, S)], [])
     emit(plan, queues, T)
     g.wait_ge(T.sem.sent, outgoing[0])

from concourse.mybir import AluOpType as Alu, ActivationFunctionType as Act

N, S, CAP = 4, 2048, 576
SLOTS = N * CAP
HALF = CAP // 2
KB = CAP // 16
KW = SLOTS // 16
UNIT = 32
BASE = 32
ROUND = 1.5 * 2.0 ** 23
PARTS = {"": (0, 18), "a": (0, 9), "b": (9, 18)}
CFG = {
    "KA": 70,
    "KB0": 32, "KB1": 88,
    "N0": 800,
    "L": (1152, 1280, 1664),
    "Y": (512, 992, 1344, 1728),
    "X1": "sB1:0:2 vF1:0:2 n0 c1:0:2 e1:0:2 vF1:2:10 sB1:2:18 sB2 sF2a vF1:10:18 vF2b p1:2:18 sB3 m0 p2 vG3 e3"
          " vS0:0:14 sB0 i0 sS0 t1:2:18 t2 vS0:14:18 vG0",
    "X2": "sB1 vF1a sB2 sF2a sB3a sB3b vF1b p1 vF2b vF3a p2 vF3b p3 sB0 sF0a sF0b n0 rv1 rv2 d0a d0b rs3",
}
SCALES = {"lp": 1.0, "ln": -1.0, "up": 32.0, "un": -32.0, "dp": 1.0 / 32}

SCRATCH = {
    "A": ("sbuf", [128, S], "bfloat16"), "B": ("sbuf", [128, S], "bfloat16"),
    "la": ("sbuf", [128, 128], "int32"), "lb": ("sbuf", [128, 128], "int32"),
    "ka": ("sbuf", [128, 128], "int32"), "kb": ("sbuf", [128, 128], "int32"),
    "fa": ("sbuf", [128, 128], "float32"), "fb": ("sbuf", [128, 128], "float32"),
    "da": ("sbuf", [128, 128], "float32"), "db": ("sbuf", [128, 128], "float32"),
    "posa": ("sbuf", [128, 128], "uint16"), "posb": ("sbuf", [128, 128], "uint16"),
    "ua": ("sbuf", [128, 128], "uint16"), "ub": ("sbuf", [128, 128], "uint16"),
    "Z": ("sbuf", [128, KW], "float32"), "zer": ("sbuf", [128, S], "bfloat16"),
    "num": ("sbuf", [128, S], "float32"),
    "Wv": ("sbuf", [128, SLOTS], "float32"),
    "Was": ("sbuf", [128, SLOTS], "float32"), "Wbs": ("sbuf", [128, SLOTS], "float32"),
    "Oav": ("sbuf", [128, KW], "float32"), "Oas": ("sbuf", [128, KW], "float32"),
    "Obv": ("sbuf", [128, KW], "float32"), "Obs": ("sbuf", [128, KW], "float32"),
    "Oa": ("sbuf", [128, KW], "float32"), "Ob": ("sbuf", [128, KW], "float32"),
    "inva": ("sbuf", [128, KW], "uint16"), "invb": ("sbuf", [128, KW], "uint16"),
    "Fn": ("sbuf", [128, S], "bfloat16"), "Fm": ("sbuf", [128, S], "bfloat16"), "Bn": ("sbuf", [128, S], "bfloat16"),
    "F1": ("sbuf", [128, SLOTS], "bfloat16"), "B1": ("sbuf", [128, SLOTS], "bfloat16"),
    "F2": ("sbuf", [128, SLOTS], "bfloat16"), "B2": ("sbuf", [128, SLOTS], "bfloat16"),
    "S1": ("sbuf", [128, N * HALF], "float16"), "S2": ("sbuf", [128, N * HALF], "float16"),
    "X1": ("sbuf", [128, N * HALF], "float16"), "X2": ("sbuf", [128, N * HALF], "float16"),
    "E": ("sbuf", [128, SLOTS], "bfloat16"), "U": ("sbuf", [128, N * HALF], "bfloat16"),
    "R1": ("sbuf", [128, SLOTS], "bfloat16"), "R2": ("sbuf", [128, SLOTS], "bfloat16"),
    "L": ("sbuf", [128, S], "bfloat16"), "Y": ("sbuf", [128, S], "bfloat16"),
    "G": ("sbuf", [128, 1024], "bfloat16"),
}
for _n in SCALES:
    SCRATCH[_n] = ("sbuf", [128, 128], "bfloat16")
for _n in ("P0", "P1", "P2", "P3", "Q0", "Q1", "Q2", "Q3"):
    SCRATCH[_n] = ("psum", [128, 512], "float32")
SEMAPHORES = ["sent"] + ["a%d_%d" % (h, k) for h in (1, 2) for k in range(5)] + ["e%d" % i for i in range(139)]


def parse(text):
    out = []
    for w in text.split():
        i = min(j for j, ch in enumerate(w) if ch.isdigit())
        rest = w[i + 1:]
        lo, hi = PARTS[rest] if rest in PARTS else [int(v) for v in rest.split(":")[1:]]
        out.append((w[:i], int(w[i]), lo * UNIT, hi * UNIT))
    return out


def new_plan():
    return {"ops": [], "acc": [], "known": {}, "groups": {}}


def add(plan, q, fn, reads=(), writes=(), inc=1, sem=None, group=None):
    ops = plan["ops"]
    me = len(ops)
    deps = set()
    for (buf, lo, hi, who, wr) in plan["acc"]:
        for (b2, l2, h2) in writes:
            if buf == b2 and lo < h2 and l2 < hi:
                deps.add(who)
        if wr:
            for (b2, l2, h2) in reads:
                if buf == b2 and lo < h2 and l2 < hi:
                    deps.add(who)
    known = plan["known"].setdefault(q, set())
    waits = []
    for d in sorted(deps, reverse=True):
        gd = ops[d]["group"]
        if d in known or (gd is not None and gd == group):
            continue
        members = plan["groups"][gd] if gd is not None else [d]
        waits.append(members[0])
        for m in members:
            known |= ops[m]["knows"]
    ops.append({"q": q, "fn": fn, "waits": waits, "knows": set(known) | {me}, "inc": inc, "sem": sem, "group": group})
    if group is not None:
        plan["groups"].setdefault(group, []).append(me)
    for (b2, l2, h2) in reads:
        plan["acc"].append((b2, l2, h2, me, False))
    for (b2, l2, h2) in writes:
        plan["acc"].append((b2, l2, h2, me, True))


def emit(plan, queues, T):
    ops = plan["ops"]
    needed = set()
    for op in ops:
        needed |= set(op["waits"])
    sems, count = {}, 0
    for i, op in enumerate(ops):
        if op["sem"] is not None:
            sems[i] = (T.sem[op["sem"][0]], op["sem"][1])
        elif i in needed:
            members = plan["groups"][op["group"]] if op["group"] is not None else [i]
            for m in members:
                sems[m] = (T.sem["e%d" % count], op["inc"] * len(members))
            count += 1
    for i, op in enumerate(ops):
        if op["q"] is None:
            continue
        eng = queues[op["q"]]
        for d in op["waits"]:
            eng.wait_ge(sems[d][0], sems[d][1])
        if op["fn"] is not None:
            ins = op["fn"](eng)
            if i in sems:
                ins.then_inc(sems[i][0], op["inc"])


def rank_program(g, core, T, topo):
    q = T.rank_of(core)
    if q is None:
        return
    C = CFG
    KA, KB0, KB1 = C["KA"], C["KB0"], C["KB1"]
    plan = new_plan()
    queues = {"g": g, "v": g.vector, "s": g.scalar, "y": g.sync, "t": g.tensor}
    outgoing = [0]

    def whole(name):
        return (name, 0, T[name].shape[1])

    def dma(queue, out, in_, reads, writes):
        add(plan, queue, lambda e: e.dma_start(out, in_), reads, writes, inc=16)

    def load(dst, src):
        dma("y", T[dst][:], src[:], [], [whole(dst)])

    def fill(queue, w):
        dma(queue, T[w][0:128:16, :], T.Z[:], [whole("Z")], [whole(w)])

    def regroup(w, o):
        dma("y", T[o][:], T[w][0:128:16, :], [whole(w)], [whole(o)])

    def memset(name, lo, hi, val):
        add(plan, "v", lambda e: e.memset(T[name][:, lo:hi], val), [], [(name, lo, hi)])

    def numbers(lo, hi):
        add(plan, "g", lambda e: e.iota(T.num[:, lo:hi], [[1, hi - lo]], BASE + lo, 0, allow_small_or_imprecise_dtypes=True),
            [], [("num", lo, hi)])

    def identity(name):
        add(plan, "g", lambda e: e.affine_select(T[name][:], T.zer[:, 0:128], [[-1, 128]], Alu.not_equal, SCALES[name], 0, 1),
            [("zer", 0, 128)], [whole(name)])

    def scalar(out, olo, src, lo, n, s1, s2, *ops):
        add(plan, "v", lambda e: e.tensor_scalar(T[out][:, olo:olo + n], T[src][:, lo:lo + n], s1, s2, *ops),
            [(src, lo, lo + n)], [(out, olo, olo + n)])

    def affine(queue, out, olo, src, lo, n, mul, plus):
        if queue == "v":
            scalar(out, olo, src, lo, n, mul, plus, Alu.mult, Alu.add)
        else:
            add(plan, "s", lambda e: e.activation(T[out][:, olo:olo + n], T[src][:, lo:lo + n], Act.Identity,
                                                  bias=plus, scale=mul), [(src, lo, lo + n)], [(out, olo, olo + n)])

    def both(out, olo, a, alo, b, blo, n, op):
        add(plan, "v", lambda e: e.tensor_tensor(T[out][:, olo:olo + n], T[a][:, alo:alo + n], T[b][:, blo:blo + n], op),
            [(a, alo, alo + n), (b, blo, blo + n)], [(out, olo, olo + n)])

    def narrow(out, src):
        add(plan, "v", lambda e: e.tensor_copy(T[out][:], T[src][:]), [whole(src)], [whole(out)])

    def position(x, step):
        if step == 0:
            scalar("k" + x, 0, "l" + x, 0, 128, 4, None, Alu.logical_shift_right)
        elif step == 1:
            scalar("f" + x, 0, "l" + x, 0, 128, KW / (SLOTS - 1.0), None, Alu.mult)
        elif step == 2:
            both("d" + x, 0, "f" + x, 0, "k" + x, 0, 128, Alu.subtract)
        else:
            affine("v", "pos" + x, 0, "d" + x, 0, 128, SLOTS - 1.0, 0.25)

    def scatter_s(w, pos, c, d):
        add(plan, "s", lambda e: e.activation(T[w][:].indirect(T[pos][:, c:d]), T.num[:, 16 * c:16 * d], Act.Silu),
            [whole(pos), ("num", 16 * c, 16 * d)], [whole(w)])

    def scatter_v(pos, c, d, sign):
        add(plan, "v", lambda e: e.tensor_scalar(T.Wv[:].indirect(T[pos][:, c:d]), T.num[:, 0:16 * (d - c)],
                                                 sign, sign * 16 * c, Alu.mult, Alu.add),
            [whole(pos), ("num", 0, 16 * (d - c))], [whole("Wv")])

    def offsets(inv, src, lo, n):
        scalar(inv, lo, src, lo, n, 0.25 - BASE, 0.0, Alu.add, Alu.max)

    def scans(src, op):
        add(plan, "v", lambda e: e.tensor_tensor_scan(T.Bn[:, S - 2::-1], T[src][:, S - 1:0:-1], T.zer[:, 0:S - 1], 0.0,
                                                      Alu.add, op), [whole(src), whole("zer")], [("Bn", 0, S - 1)])
        add(plan, "v", lambda e: e.tensor_tensor_scan(T.Fn[:, 1:S], T[src][:, 0:S - 1], T.zer[:, 0:S - 1], 0.0,
                                                      Alu.add, op), [whole(src), whole("zer")], [("Fn", 1, S)])

    def capped(h, queue, which, inv, lo, hi, scale):
        src, out = which + "n", which + str(h)
        o, win = T[out][:, lo:hi], T[src][:, 0:S].indirect(T[inv][:, lo // 16:hi // 16])
        if queue == "s":
            fn = lambda e: e.activation(o, win, Act.Relu, bias=15.0, scale=-1.0 if h == 1 else 1.0)
        elif h == 1:
            fn = lambda e: e.tensor_scalar(o, win, 15.0, -scale, Alu.min, Alu.mult)
        else:
            fn = lambda e: e.tensor_scalar(o, win, -15.0, -scale, Alu.max, Alu.mult)
        add(plan, queue, fn, [whole(src), (inv, lo // 16, hi // 16)], [(out, lo, hi)])

    def gathered(out, win, off, other, lo, hi, op):
        add(plan, "v", lambda e: e.tensor_tensor(T[out][:, lo:hi], T[win][:].indirect(T[off][:, lo // 16:hi // 16]),
                                                 T[other][:, lo:hi], op),
            [whole(win), (off, lo // 16, hi // 16), (other, lo, hi)], [(out, lo, hi)])

    def matmul(bank, n, mat, src, lo, start, stop, group):
        add(plan, "t", lambda e: e.matmul(T[bank][:, 0:n], T[mat][:], T[src][:, lo:lo + n], start, stop),
            [whole(mat), (src, lo, lo + n)], [whole(bank)], group=group)

    def send(k, sem, src, slo, land, dlo, n):
        dst = T.cores[(q + k) % N]
        rid, pid = topo.addr(dst, core)
        outgoing[0] += len(topo.engines(core, dst))
        add(plan, "g", lambda e: e.remote_dma(T[land][:, dlo:dlo + n], T[src][:, slo:slo + n], T.sem[sem], T.sem.sent,
                                              pid, rid, topo.mask(core, dst)), [(src, slo, slo + n)], [])

    def exchange(h, inv, extra):
        steps = parse(C["X%d" % h])
        f, b, sbuf, x, out = ("%s%d" % (n, h) for n in "FBSXR")
        carried = 15.0 * (2 * h - 3)
        sends = [(k, lo, hi) for what, k, lo, hi in steps if what in "pe"]
        fine = [(k, lo, hi) for what, k, lo, hi in steps if what == "t"]
        pending, by, bank, arrived, turn = [], {}, {}, [], [0]
        for what, k, lo, hi in steps:
            mid = (lo + hi) // 2
            if what == "p":
                up, low = ("l", "d") if (k, lo, hi) in fine else ("u", "l")
                pending += [((k, lo, hi), "F", lo, mid, up), ((k, lo, hi), "B", lo, mid, up), ((k, lo, hi), "B", mid, hi, low)]
            elif what == "d":
                pending += [((k, lo, hi), "F", lo, hi, "l"), ((k, lo, hi), "B", lo, hi, "l")]

        def next_bank():
            turn[0] += 1
            return "Q%d" % (turn[0] % N)

        def arrive(k, lo, hi, buf, c, n):
            arrived.append((k, lo, hi))
            count = len(topo.engines(T.cores[(q - k) % N], core))
            add(plan, None, None, [], [(buf, c, c + n)], sem=("a%d_%d" % (h, sends.index((k, lo, hi))), count))

        for what, k, lo, hi in steps:
            piece, mid, n = (k, lo, hi), (lo + hi) // 2, (hi - lo) // 2
            to, fro = (q + k) % N * CAP, (q - k) % N * CAP
            made = "E" if k else out
            if what in extra:
                extra[what](lo, hi)
            elif what == "p":
                both(sbuf, (to + lo) // 2, bank[piece], 0, f, to + mid, n, Alu.add)
                send(k, "a%d_%d" % (h, sends.index(piece)), sbuf, (to + lo) // 2, x, (q * CAP + lo) // 2, n)
            elif what == "e":
                send(k, "a%d_%d" % (h, sends.index(piece)), "E", to + lo, out, q * CAP + lo, hi - lo)
            elif what == "c":
                both(made, to + lo, f, to + lo, b, to + lo, hi - lo, Alu.add)
            elif what == "d":
                affine("s", made, to + lo, bank[piece], 0, hi - lo, 1.0, carried if by[("F", k, lo)] == "s" else 0.0)
            elif what == "m":
                scalar("Fm", 0, "Fn", 0, S, 15.0, -1.0, Alu.min, Alu.mult)
            elif what == "vG":
                gathered(made, "Fm", inv, b, to + lo, to + hi, Alu.add)
            elif what[0] in "rt":
                c, a, lack = (fro + lo) // 2, fro + lo, carried if by[("F", k, lo)] == "s" else 0.0
                arrive(k, lo, hi, x, c, n)
                if what[0] == "r":
                    scalar("U", c, x, c, n, 32 * ROUND, 32 * ROUND, Alu.add, Alu.subtract)
                    affine(what[1], out, a, "U", c, n, 1.0 / 32, lack)
                    both(out, fro + mid, x, c, "U", c, n, Alu.subtract)
                else:
                    p = next_bank()
                    matmul(p, n, "up", x, c, True, False, ("split", h, piece))
                    scalar(out, a, x, c, n, ROUND, ROUND - lack, Alu.add, Alu.subtract)
                    matmul(p, n, "un", out, a, False, True, ("split", h, piece))
                    affine("s", out, fro + mid, p, 0, n, 1.0, 32 * lack)
            else:
                small = what == "vF" and any(kk == k and (a + z) // 2 <= lo and hi <= z for kk, a, z in fine)
                capped(h, what[0], what[1], inv, to + lo, to + hi, 1.0 / 32 if small else 1.0)
                for c in range(lo, hi, UNIT):
                    by[(what[1], k, c)] = what[0]
                for term in list(pending):
                    pc, which, a, z, weight = term
                    if all((which, pc[0], c) in by for c in range(a, z, UNIT)):
                        pending.remove(term)
                        first = pc not in bank
                        if first:
                            bank[pc] = next_bank()
                        sign = "p" if h == 1 or by[(which, pc[0], a)] == "v" else "n"
                        matmul(bank[pc], z - a, weight + sign, which + str(h), (q + pc[0]) % N * CAP + a, first,
                               not any(t[0] == pc for t in pending), ("sum", h, pc))
        for k, lo, hi in sends:
            if (k, lo, hi) not in arrived:
                arrive(k, lo, hi, out, (q - k) % N * CAP + lo, hi - lo)

    def channel_in(src, mat, banks, cuts):
        for p, lo, hi in zip(banks, cuts, cuts[1:]):
            matmul(p, hi - lo, mat, src, lo, True, False, p)

    def gather_s(out, rbuf, off, banks, cuts):
        for p, lo, hi in zip(banks, cuts, cuts[1:]):
            c = lo - cuts[0]
            add(plan, "s", lambda e, c=c, lo=lo, hi=hi: e.activation(
                T.G[:, c:c + hi - lo], T[rbuf][:].indirect(T[off][:, lo // 16:hi // 16]), Act.Copy),
                [whole(rbuf), whole(off)], [("G", c, c + hi - lo)])
            matmul(p, hi - lo, "lp", "G", c, False, True, p)
        for p, lo, hi in zip(banks, cuts, cuts[1:]):
            affine("s", out, lo, p, 0, hi - lo, 1.0, 0.0)

    n0, n1 = C["N0"], 16 * KA
    lcut, ycut = list(C["L"]) + [S], [0] + list(C["Y"]) + [S]
    load("la", T.sa)
    load("lb", T.sb)
    numbers(0, n0)
    memset("Z", 0, KW, 0.0)
    fill("s", "Was")
    fill("y", "Wv")
    add(plan, "s", lambda e: e.activation(T.Bn[:, S - 1:S], T.Z[:, 0:1], Act.Silu), [whole("Z")], [("Bn", S - 1, S)])
    load("A", T.a)
    affine("s", "num", n0, "num", 0, n1 - n0, 1.0, float(n0))
    fill("y", "Wbs")
    memset("zer", 0, S, 0.0)
    memset("Fn", 0, 1, 0.0)
    numbers(n1, 16 * KB1)
    for name in SCALES:
        identity(name)

    for x, step in (("a", 0), ("a", 1), ("b", 0), ("a", 2), ("b", 1), ("a", 3), ("b", 2)):
        position(x, step)
    scatter_s("Was", "posa", 0, KA)
    scatter_v("posa", KA, 128, -1.0)
    position("b", 3)
    regroup("Wv", "Oav")
    regroup("Was", "Oas")
    load("B", T.b)
    scatter_s("Wbs", "posb", 0, KB0)
    channel_in("A", "lp", ["P2", "P3"], ycut[-3:])
    scans("A", Alu.max)
    halves = [0, KW // 2] if (q + 1) % N < N // 2 else [KW // 2, 0]
    for lo in halves:
        both("Oa", lo, "Oas", lo, "Oav", lo, KW // 2, Alu.subtract)
    for lo in halves:
        offsets("inva", "Oa", lo, KW // 2)

    def rest_s(lo, hi):
        scatter_s("Wbs", "posb", KB0, KB1)
        regroup("Wbs", "Obs")

    def rest_v(lo, hi):
        c, d = (KB1 + (128 - KB1) * v // CAP // 2 * 2 for v in (lo, hi))
        scatter_v("posb", c, d, 1.0)
        if hi == CAP:
            regroup("Wv", "Obv")
    exchange(1, "inva", {"n": lambda lo, hi: narrow("ub", "lb"), "sS": rest_s, "vS": rest_v,
                         "i": lambda lo, hi: channel_in("B", "ln", ["P0", "P1"], lcut[-3:])})

    gathered("L", "R1", "ub", "B", 0, lcut[0], Alu.subtract)
    gather_s("L", "R1", "ub", ["P0", "P1"], lcut[-3:])
    both("Ob", 0, "Obs", 0, "Obv", 0, KW, Alu.max)
    gathered("L", "R1", "ub", "B", lcut[0], lcut[1], Alu.subtract)
    offsets("invb", "Ob", 0, KW)
    scans("L", Alu.min)
    exchange(2, "invb", {"n": lambda lo, hi: narrow("ua", "la")})

    for lo, hi in zip(ycut[:3], ycut[1:4]):
        gathered("Y", "R2", "ua", "A", lo, hi, Alu.add)
    gather_s("Y", "R2", "ua", ["P2", "P3"], ycut[-3:])
    for lo, hi in ((0, ycut[1]), (ycut[1], ycut[2]), (ycut[2], S)):
        dma("y", T.y[:, lo:hi], T.Y[:, lo:hi], [("Y", lo, hi)], [("y", lo, hi)])
    add(plan, "y", None, [("y", 0, S)], [])
    emit(plan, queues, T)
    g.wait_ge(T.sem.sent, outgoing[0])
